import numpy as np
import ml_dtypes


def mxq(x, axis, fmt="e4m3"):
    dtype, down = {"e4m3": (ml_dtypes.float8_e4m3fn, 7), "e5m2": (ml_dtypes.float8_e5m2, 14)}[fmt]
    v = np.moveaxis(np.asarray(x, np.float32).astype(ml_dtypes.bfloat16).astype(np.float64), axis, -1)
    blocks = v.reshape(v.shape[:-1] + (-1, 32))
    amax = np.abs(blocks).max(-1, keepdims=True)
    byte = np.maximum(np.where(amax > 0, np.frexp(amax)[1] - 1 + 127, 0) - down, 1)
    scale = np.exp2(byte - 127.0)
    codes = (blocks / scale).astype(np.float32).astype(dtype).astype(np.float64)
    return np.moveaxis((codes * scale).reshape(v.shape), -1, axis)


WIDE = False


def mx_kscale(k):
    if not WIDE:
        return np.ones(k)
    levels = np.array([10, -10, 5, -5, 0])
    if k % 512:
        return np.exp2(np.random.permutation(np.resize(levels, k // 32))).repeat(32)
    a = np.empty((k // 512, 16))
    for p in range(k // 512):
        a[p, :8] = np.random.permutation(np.resize(levels, 8))
        for g in range(8):
            far = levels[np.abs(levels - a[p, g]) >= 10]
            a[p, g + 8] = far[np.random.randint(len(far))]
    return np.exp2(a.ravel()).repeat(32)


def f64(x):
    return np.asarray(x).astype(np.float64)


def striped(idx):
    return np.tile(np.asarray(idx).reshape(-1, 16).T, (8, 1)).astype(np.uint16)


def unstriped(offs):
    return offs[:16].T.reshape(-1).astype(np.int64)


E2M1 = np.array([0.0, 0.5, 1.0, 1.5, 2.0, 3.0, 4.0, 6.0, -0.0, -0.5, -1.0, -1.5, -2.0, -3.0, -4.0, -6.0])


def pack_weight(w, fmt):
    k, n = w.shape
    w = f64(np.asarray(w, np.float32).astype(ml_dtypes.bfloat16)).reshape(k // 32, 32, n)
    amax = np.abs(w).max(1)
    if fmt == "e4m3":
        byte = np.frexp(amax)[1] - 1 + 127 - 7
    else:
        mant, ex = np.frexp(amax / 6.0)
        byte = np.where(mant > 0.5, ex, ex - 1) + 127
    byte = np.clip(np.where(amax > 0, byte, 1), 1, 254)
    scaled = (w * np.exp2(127.0 - byte)[:, None, :]).reshape(k, n).astype(np.float32)
    by_word = np.ascontiguousarray(scaled.reshape(k // 512, 128, 4, n).transpose(0, 1, 3, 2))
    if fmt == "e4m3":
        words = by_word.astype(ml_dtypes.float8_e4m3fn).view(np.uint8)
    else:
        c = by_word.astype(ml_dtypes.float4_e2m1fn).view(np.uint8) & 0xF
        words = (c[..., 0::2] | (c[..., 1::2] << 4)).reshape(k // 512, 128, 2 * n)
    return np.ascontiguousarray(words), np.ascontiguousarray(byte.astype(np.uint8).reshape(k // 512, 16, n))


def unpack_weight(words, scales, fmt):
    g, _, n = scales.shape
    words = np.ascontiguousarray(words).reshape(g, 128, n, -1)
    if fmt == "e4m3":
        vals = words.view(ml_dtypes.float8_e4m3fn).astype(np.float64)
    else:
        nib = np.empty((g, 128, n, 4), np.uint8)
        nib[..., 0::2] = words & 0xF
        nib[..., 1::2] = words >> 4
        vals = E2M1[nib]
    vals = vals * np.repeat(np.exp2(scales.astype(np.float64) - 127.0), 8, axis=1)[..., None]
    return vals.transpose(0, 1, 3, 2).reshape(g * 512, n)


B, N, T, D, DV, NQ = 1, 1024, 4096, 512, 128, 128
CAP = 2.0


def setup_inputs():
    n = np.random.standard_normal
    idx = np.sort(np.random.permutation(T)[:B * N].reshape(B, N), axis=1).reshape(-1)
    s = mx_kscale(D)[:, None]
    u = np.ones(T)
    u[idx] = mx_kscale(B * N)
    r = np.random.uniform(0.5, 2.0, T)
    qp = [pack_weight(x, "e4m3") for x in n((B, D, NQ)) * s * (0.60 / np.sqrt(D))]
    k = n((D, T)) / s
    v = n((DV, T)) / (u * r)
    kp = pack_weight(k, "e4m3")
    return {
        "q_words": np.stack([x[0] for x in qp]),
        "q_scales": np.stack([x[1] for x in qp]),
        "k_words": kp[0],
        "k_scales": kp[1],
        "vT": v.astype(np.float32),
        "vs": np.tile(u * r, (128, 1)).astype(np.float32),
        "offs": striped(idx),
    }


def reference(q_words, q_scales, k_words, k_scales, vT, vs, offs):
    idx = unstriped(offs)
    k = unpack_weight(k_words, k_scales, "e4m3")
    v = f64(vT)
    pick = lambda x: x[:, idx].reshape(x.shape[0], B, N).transpose(1, 0, 2)
    q = np.stack([unpack_weight(q_words[b], q_scales[b], "e4m3") for b in range(B)])
    score = q.transpose(0, 2, 1) @ pick(k)
    score = CAP * np.tanh(score / CAP)
    m = score.max(-1, keepdims=True)
    p = np.exp(score - m)
    total = p.sum(-1, keepdims=True)
    w = p * pick(f64(vs))[:, :1, :]
    y = mxq(w, 2, "e4m3") @ mxq(pick(v).transpose(0, 2, 1), 1, "e4m3")
    y = y / total
    return y

@@ -1,0 +1,174 @@
+from contextlib import ExitStack
+
+import concourse.mybir as mybir
+from concourse.masks import make_identity
+
+P = 128
+T = 4096
+N = 1024
+D = 512
+DV = 128
+NQ = 128
+CAP = 2.0
+PACK = 4
+PASS = P * PACK
+PASSES = N // PASS
+LIST_COLS = PASS // 16
+
+FLOPS = 2 * NQ * N * (D + DV)
+
+F32 = mybir.dt.float32
+BF16 = mybir.dt.bfloat16
+I32 = mybir.dt.int32
+U32 = mybir.dt.uint32
+U16 = mybir.dt.uint16
+U8 = mybir.dt.uint8
+FP8X4 = mybir.dt.float8_e4m3fn_x4
+ACT = mybir.ActivationFunctionType
+ALU = mybir.AluOpType
+
+
+def tile_attend_qpk_cap_srt_kernel(tc, q_words, q_scales, k_words, k_scales, vT, vs, offs, out):
+    nc = tc.nc
+    with ExitStack() as ctx:
+        held = ctx.enter_context(tc.tile_pool(name="held", bufs=1))
+        psum = ctx.enter_context(tc.psum_pool(name="psum", bufs=1))
+
+        offsets = held.tile([P, N // 16], U16, name="offsets")
+        nc.sync.dma_start(offsets[:], offs)
+
+        def reach(g):
+            return T - (N - (g + 1) * PASS)
+
+        def slots(g):
+            return offsets[:, g * LIST_COLS : (g + 1) * LIST_COLS]
+
+        k_pool = held.tile([P, T], I32, name="k_pool", align_bytes=64)
+        nc.sync.dma_start(k_pool[:], k_words[0].rearrange("p n t -> p (n t)").bitcast(I32))
+        q_codes = held.tile([P, NQ], I32, name="q_codes", align_bytes=64)
+        nc.sync.dma_start(q_codes[:], q_words[0, 0].rearrange("p n t -> p (n t)").bitcast(I32))
+
+        ks_pool = held.tile([P, T], U8, name="ks_pool", align_bytes=64)
+        nc.vector.memset(ks_pool[:].bitcast(I32), 0)
+        vs_pool = held.tile([P, T], F32, name="vs_pool", align_bytes=64)
+        nc.vector.memset(vs_pool[0 : P - 1, 0:PASS], 0.0)
+        nc.vector.memset(vs_pool[0 : P - 1, PASS:T], 0.0)
+        q_plane = held.tile([P, NQ], U8, name="q_plane", align_bytes=64)
+        nc.vector.memset(q_plane[:].bitcast(I32), 0)
+
+        nc.scalar.dma_start(vs_pool[P - 1 : P, :], vs[0:1, :])
+        for r in range(4):
+            nc.scalar.dma_start(ks_pool[r:P:32, :].bitcast(I32), k_scales[0, r:16:4, :].bitcast(I32))
+        warm = held.tile([P, 1], F32, name="warm", tag="v_pool", align_bytes=64)
+        nc.scalar.activation(warm[0:64, :], vs_pool[0:64, 0:1], ACT.Exp)
+        for r in range(4):
+            nc.scalar.dma_start(q_plane[r:P:32, :].bitcast(I32), q_scales[0, 0, r:16:4, :].bitcast(I32))
+
+        v_pool = held.tile([P, T], F32, name="v_pool", tag="v_pool", align_bytes=64)
+        for lo, hi in ((0, 2560), (2560, 3072), (3072, 3584), (3584, 4096)):
+            nc.sync.dma_start(v_pool[:, lo:hi], vT[:, lo:hi])
+
+        ident = held.tile([P, P], F32, name="ident", align_bytes=64)
+        make_identity(nc, ident[:])
+
+        vs_slot = []
+        for g in range(PASSES):
+            vs_row = held.tile([P, PASS], F32, name="vs_row%d" % g, align_bytes=64)
+            nc.vector.tensor_copy(vs_row[:], vs_pool[:].indirect(slots(g)))
+            vs_turned = psum.tile([P, PACK, P], F32, name="vs_turned%d" % g, tag="turn%d" % g)
+            for t in range(PACK):
+                nc.tensor.transpose(vs_turned[:, t, :], vs_row[:, t:PASS:PACK], ident[:])
+            col = held.tile([P, PACK], F32, name="vs_slot%d" % g)
+            nc.scalar.copy(col[:], vs_turned[:, :, P - 1])
+            vs_slot.append(col)
+
+        k_plane = held.tile([P, N], U8, name="k_plane", align_bytes=64)
+        nc.vector.tensor_copy(k_plane[:], ks_pool[:].indirect(offsets[:]))
+
+        tanh_half = []
+        for g in range(PASSES):
+            k_codes = held.tile([P, PASS], I32, name="k_codes%d" % g, align_bytes=64)
+            nc.vector.tensor_copy(k_codes[:].bitcast(U32), k_pool[:].bitcast(U32).indirect(slots(g)))
+            score = psum.tile([P, PASS], F32, name="score%d" % g)
+            nc.tensor.matmul_mx(
+                out=score[:],
+                lhsT=q_codes[:].bitcast(FP8X4),
+                lhsT_scale=q_plane[:],
+                rhs=k_codes[:].bitcast(FP8X4),
+                rhs_scale=k_plane[:, g * PASS : (g + 1) * PASS],
+                start=True,
+                stop=True,
+            )
+            th = held.tile([P, PACK, P], F32, name="tanh%d" % g, tag="tanh%d" % g, align_bytes=64)
+            nc.scalar.activation(th[:], score[:].rearrange("q (s t) -> q t s", t=PACK), ACT.Tanh, scale=1.0 / CAP)
+            tanh_half.append(th)
+
+        neg_c = []
+        neg_m = None
+        for g in range(PASSES):
+            nc_g = held.tile([P, PASS], F32, name="neg_c%d" % g, align_bytes=64)
+            least = held.tile([P, 1], F32, name="neg_m%d" % g)
+            nc.vector.tensor_scalar(
+                nc_g[:], tanh_half[g][:].rearrange("q t s -> q (t s)"), -CAP, neg_m, ALU.mult, ALU.min, accum_out=least[:]
+            )
+            neg_m = least[:]
+            neg_c.append(nc_g)
+
+        turned = []
+        sums = []
+        for g in range(PASSES):
+            p = held.tile([P, PASS], F32, name="p%d" % g, align_bytes=64)
+            total = held.tile([P, 1], F32, name="sum%d" % g)
+            nc.scalar.activation(p[:], neg_c[g][:], ACT.Exp, bias=neg_m, scale=-1.0, accum_out=total[:])
+            sums.append(total)
+            p_turned = psum.tile([P, PACK, P], F32, name="p_turned%d" % g, tag="turn%d" % g)
+            for t in range(PACK):
+                nc.tensor.transpose(p_turned[:, t, :], p[:, t * P : (t + 1) * P], ident[:])
+            turned.append(p_turned)
+        row_sum = held.tile([P, 1], F32, name="row_sum")
+        nc.scalar.activation(row_sum[:], sums[0][:], ACT.Identity, bias=sums[1][:], scale=1.0)
+
+        wv = []
+        v_all = held.tile([P, N], BF16, name="v_all", tag="tanh%d" % (PASSES - 1), align_bytes=64)
+        for g in range(PASSES):
+            both = held.tile([P, 2 * PASS], BF16, name="wv%d" % g, align_bytes=64)
+            wv.append(both)
+            v_pairs = v_all[:, g * PASS : (g + 1) * PASS]
+            nc.vector.tensor_copy(
+                v_pairs.rearrange("e (u s h) -> e s u h", u=2, h=2), v_pool[:, 0 : reach(g)].indirect(slots(g))
+            )
+            v_turned = psum.tile([P, 2, P], F32, name="v_turned%d" % g)
+            for u in range(2):
+                nc.tensor.transpose(v_turned[:, u, :], v_pairs.bitcast(F32)[:, u * P : (u + 1) * P], ident[:])
+            nc.scalar.copy(
+                both[:, PASS : 2 * PASS].bitcast(F32).rearrange("s (e u) -> s e u", u=2), v_turned[:].rearrange("s u e -> s e u")
+            )
+
+        inv_sum = held.tile([P, 1], F32, name="inv_sum")
+        nc.vector.reciprocal(inv_sum[:], row_sum[:])
+        for g in range(PASSES):
+            nc.vector.tensor_tensor(
+                wv[g][:, 0:PASS].rearrange("s (q t) -> s q t", t=PACK),
+                turned[g][:].rearrange("s t q -> s q t"),
+                vs_slot[g][:].unsqueeze(1).to_broadcast([P, NQ, PACK]),
+                ALU.mult,
+            )
+
+        acc = psum.tile([P, DV], F32, name="acc")
+        for g in range(PASSES):
+            codes = held.tile([P, 2 * P], U32, name="codes%d" % g, align_bytes=64)
+            plane = held.tile([P, 2 * P], U8, name="plane%d" % g, align_bytes=64)
+            nc.vector.quantize_mx(out=codes[:].bitcast(FP8X4), scales=plane[:], in_=wv[g][:])
+            nc.tensor.matmul_mx(
+                out=acc[:],
+                lhsT=codes[:, 0:P].bitcast(FP8X4),
+                lhsT_scale=plane[:, 0:P],
+                rhs=codes[:, P : 2 * P].bitcast(FP8X4),
+                rhs_scale=plane[:, P : 2 * P],
+                start=(g == 0),
+                stop=(g == PASSES - 1),
+            )
+
+        result = held.tile([P, DV], F32, name="result", align_bytes=64)
+        nc.scalar.activation(result[:], acc[:], ACT.Copy, scale=inv_sum[:])
+        nc.sync.dma_start(out[0], result[:])

@@ -43,30 +43,30 @@ def tile_attend_qpk_cap_srt_kernel(tc, q_words, q_scales, k_words, k_scales, vT,
         def slots(g):
             return offsets[:, g * LIST_COLS : (g + 1) * LIST_COLS]
 
-        k_pool = held.tile([P, T], I32, name="k_pool", align_bytes=64)
-        nc.sync.dma_start(k_pool[:], k_words[0].rearrange("p n t -> p (n t)").bitcast(I32))
-        q_codes = held.tile([P, NQ], I32, name="q_codes", align_bytes=64)
-        nc.sync.dma_start(q_codes[:], q_words[0, 0].rearrange("p n t -> p (n t)").bitcast(I32))
-
-        ks_pool = held.tile([P, T], U8, name="ks_pool", align_bytes=64)
+        ks_pool = held.tile([P, T], U8, name="ks_pool", tag="ks_pool", align_bytes=64)
         nc.vector.memset(ks_pool[:].bitcast(I32), 0)
         vs_pool = held.tile([P, T], F32, name="vs_pool", align_bytes=64)
-        nc.vector.memset(vs_pool[0 : P - 1, 0:PASS], 0.0)
-        nc.vector.memset(vs_pool[0 : P - 1, PASS:T], 0.0)
+        nc.vector.memset(vs_pool[0 : P - 1, 0:64], 0.0)
         q_plane = held.tile([P, NQ], U8, name="q_plane", align_bytes=64)
         nc.vector.memset(q_plane[:].bitcast(I32), 0)
+        nc.vector.memset(vs_pool[0 : P - 1, 64:T], 0.0)
 
-        nc.scalar.dma_start(vs_pool[P - 1 : P, :], vs[0:1, :])
+        nc.sync.dma_start(vs_pool[P - 1 : P, :], vs[0:1, :])
+        k_pool = held.tile([P, T], I32, name="k_pool", align_bytes=64)
+        k_all = k_words[0].rearrange("p n t -> p (n t)").bitcast(I32)
+        v_pool = held.tile([P, T], F32, name="v_pool", tag="v_pool", align_bytes=64)
+        for pool_tile, source in ((k_pool, k_all), (v_pool, vT)):
+            nc.sync.dma_start(pool_tile[:, 0 : reach(0)], source[:, 0 : reach(0)])
+            nc.sync.dma_start(pool_tile[:, reach(0) : T], source[:, reach(0) : T])
+
+        q_codes = held.tile([P, NQ], I32, name="q_codes", align_bytes=64)
+        nc.scalar.dma_start(q_codes[:], q_words[0, 0].rearrange("p n t -> p (n t)").bitcast(I32))
         for r in range(4):
             nc.scalar.dma_start(ks_pool[r:P:32, :].bitcast(I32), k_scales[0, r:16:4, :].bitcast(I32))
-        warm = held.tile([P, 1], F32, name="warm", tag="v_pool", align_bytes=64)
+        warm = held.tile([P, 1], F32, name="warm")
         nc.scalar.activation(warm[0:64, :], vs_pool[0:64, 0:1], ACT.Exp)
         for r in range(4):
             nc.scalar.dma_start(q_plane[r:P:32, :].bitcast(I32), q_scales[0, 0, r:16:4, :].bitcast(I32))
-
-        v_pool = held.tile([P, T], F32, name="v_pool", tag="v_pool", align_bytes=64)
-        for lo, hi in ((0, 2560), (2560, 3072), (3072, 3584), (3584, 4096)):
-            nc.sync.dma_start(v_pool[:, lo:hi], vT[:, lo:hi])
 
         ident = held.tile([P, P], F32, name="ident", align_bytes=64)
         make_identity(nc, ident[:])
@@ -85,16 +85,17 @@ def tile_attend_qpk_cap_srt_kernel(tc, q_words, q_scales, k_words, k_scales, vT,
         k_plane = held.tile([P, N], U8, name="k_plane", align_bytes=64)
         nc.vector.tensor_copy(k_plane[:], ks_pool[:].indirect(offsets[:]))
 
+        k_listed = held.tile([P, N], I32, name="k_listed", tag="ks_pool", align_bytes=64)
         tanh_half = []
         for g in range(PASSES):
-            k_codes = held.tile([P, PASS], I32, name="k_codes%d" % g, align_bytes=64)
-            nc.vector.tensor_copy(k_codes[:].bitcast(U32), k_pool[:].bitcast(U32).indirect(slots(g)))
+            k_codes = k_listed[:, g * PASS : (g + 1) * PASS]
+            nc.vector.tensor_copy(k_codes.bitcast(U32), k_pool[:, 0 : reach(g)].bitcast(U32).indirect(slots(g)))
             score = psum.tile([P, PASS], F32, name="score%d" % g)
             nc.tensor.matmul_mx(
                 out=score[:],
                 lhsT=q_codes[:].bitcast(FP8X4),
                 lhsT_scale=q_plane[:],
-                rhs=k_codes[:].bitcast(FP8X4),
+                rhs=k_codes.bitcast(FP8X4),
                 rhs_scale=k_plane[:, g * PASS : (g + 1) * PASS],
                 start=True,
                 stop=True,
@@ -128,37 +129,39 @@ def tile_attend_qpk_cap_srt_kernel(tc, q_words, q_scales, k_words, k_scales, vT,
         row_sum = held.tile([P, 1], F32, name="row_sum")
         nc.scalar.activation(row_sum[:], sums[0][:], ACT.Identity, bias=sums[1][:], scale=1.0)
 
-        wv = []
         v_all = held.tile([P, N], BF16, name="v_all", tag="tanh%d" % (PASSES - 1), align_bytes=64)
+        v_turned = []
         for g in range(PASSES):
-            both = held.tile([P, 2 * PASS], BF16, name="wv%d" % g, align_bytes=64)
-            wv.append(both)
             v_pairs = v_all[:, g * PASS : (g + 1) * PASS]
             nc.vector.tensor_copy(
                 v_pairs.rearrange("e (u s h) -> e s u h", u=2, h=2), v_pool[:, 0 : reach(g)].indirect(slots(g))
             )
-            v_turned = psum.tile([P, 2, P], F32, name="v_turned%d" % g)
+            bank = psum.tile([P, 2, P], F32, name="v_turned%d" % g)
             for u in range(2):
-                nc.tensor.transpose(v_turned[:, u, :], v_pairs.bitcast(F32)[:, u * P : (u + 1) * P], ident[:])
-            nc.scalar.copy(
-                both[:, PASS : 2 * PASS].bitcast(F32).rearrange("s (e u) -> s e u", u=2), v_turned[:].rearrange("s u e -> s e u")
-            )
+                nc.tensor.transpose(bank[:, u, :], v_pairs.bitcast(F32)[:, u * P : (u + 1) * P], ident[:])
+            v_turned.append(bank)
 
-        inv_sum = held.tile([P, 1], F32, name="inv_sum")
-        nc.vector.reciprocal(inv_sum[:], row_sum[:])
+        late = held.tile([P, 2 * N + 2], BF16, name="late", tag="v_pool", align_bytes=64)
+        wv = [late[:, 2 * PASS * g : 2 * PASS * (g + 1)] for g in range(PASSES)]
+        inv_sum = late[:, 2 * N : 2 * N + 2].bitcast(F32)
         for g in range(PASSES):
+            nc.scalar.copy(
+                wv[g][:, PASS : 2 * PASS].bitcast(F32).rearrange("s (e u) -> s e u", u=2),
+                v_turned[g][:].rearrange("s u e -> s e u"),
+            )
             nc.vector.tensor_tensor(
                 wv[g][:, 0:PASS].rearrange("s (q t) -> s q t", t=PACK),
                 turned[g][:].rearrange("s t q -> s q t"),
                 vs_slot[g][:].unsqueeze(1).to_broadcast([P, NQ, PACK]),
                 ALU.mult,
             )
+        nc.vector.reciprocal(inv_sum, row_sum[:])
 
         acc = psum.tile([P, DV], F32, name="acc")
         for g in range(PASSES):
             codes = held.tile([P, 2 * P], U32, name="codes%d" % g, align_bytes=64)
             plane = held.tile([P, 2 * P], U8, name="plane%d" % g, align_bytes=64)
-            nc.vector.quantize_mx(out=codes[:].bitcast(FP8X4), scales=plane[:], in_=wv[g][:])
+            nc.vector.quantize_mx(out=codes[:].bitcast(FP8X4), scales=plane[:], in_=wv[g])
             nc.tensor.matmul_mx(
                 out=acc[:],
                 lhsT=codes[:, 0:P].bitcast(FP8X4),
@@ -170,5 +173,5 @@ def tile_attend_qpk_cap_srt_kernel(tc, q_words, q_scales, k_words, k_scales, vT,
             )
 
         result = held.tile([P, DV], F32, name="result", align_bytes=64)
-        nc.scalar.activation(result[:], acc[:], ACT.Copy, scale=inv_sum[:])
+        nc.scalar.activation(result[:], acc[:], ACT.Copy, scale=inv_sum)
         nc.sync.dma_start(out[0], result[:])

@@ -44,43 +44,47 @@ def tile_attend_qpk_cap_srt_kernel(tc, q_words, q_scales, k_words, k_scales, vT,
             return offsets[:, g * LIST_COLS : (g + 1) * LIST_COLS]
 
         ks_pool = held.tile([P, T], U8, name="ks_pool", tag="ks_pool", align_bytes=64)
-        nc.vector.memset(ks_pool[:].bitcast(I32), 0)
-        vs_pool = held.tile([P, T], F32, name="vs_pool", align_bytes=64)
-        nc.vector.memset(vs_pool[0 : P - 1, 0:64], 0.0)
+        nc.gpsimd.memset(ks_pool[:].bitcast(I32), 0)
         q_plane = held.tile([P, NQ], U8, name="q_plane", align_bytes=64)
-        nc.vector.memset(q_plane[:].bitcast(I32), 0)
-        nc.vector.memset(vs_pool[0 : P - 1, 64:T], 0.0)
+        nc.gpsimd.memset(q_plane[:].bitcast(I32), 0)
+        vs_pool = held.tile([P, T], F32, name="vs_pool", align_bytes=64)
+        nc.vector.memset(vs_pool[0 : P - 1, 0:63], 0.0)
+        nc.vector.memset(vs_pool[0 : P - 1, 63:2368], 0.0)
+        nc.gpsimd.memset(vs_pool[0 : P - 1, 2368:T], 0.0)
 
-        nc.sync.dma_start(vs_pool[P - 1 : P, :], vs[0:1, :])
-        k_pool = held.tile([P, T], I32, name="k_pool", align_bytes=64)
-        k_all = k_words[0].rearrange("p n t -> p (n t)").bitcast(I32)
-        v_pool = held.tile([P, T], F32, name="v_pool", tag="v_pool", align_bytes=64)
-        for pool_tile, source in ((k_pool, k_all), (v_pool, vT)):
+        warm = held.tile([P, 1], F32, name="warm")
+        nc.scalar.activation(warm[0:64, :], vs_pool[0:64, 0:1], ACT.Exp)
+
+        def load_pool(pool_tile, source):
             nc.sync.dma_start(pool_tile[:, 0 : reach(0)], source[:, 0 : reach(0)])
             nc.sync.dma_start(pool_tile[:, reach(0) : T], source[:, reach(0) : T])
 
+        nc.sync.dma_start(vs_pool[P - 1 : P, :], vs[0:1, :])
+        for r in range(4):
+            nc.sync.dma_start(ks_pool[r:P:32, :].bitcast(I32), k_scales[0, r:16:4, :].bitcast(I32))
+        k_pool = held.tile([P, T], I32, name="k_pool", tag="k_pool", align_bytes=64)
+        load_pool(k_pool, k_words[0].rearrange("p n t -> p (n t)").bitcast(I32))
         q_codes = held.tile([P, NQ], I32, name="q_codes", align_bytes=64)
-        nc.scalar.dma_start(q_codes[:], q_words[0, 0].rearrange("p n t -> p (n t)").bitcast(I32))
+        nc.sync.dma_start(q_codes[:], q_words[0, 0].rearrange("p n t -> p (n t)").bitcast(I32))
         for r in range(4):
-            nc.scalar.dma_start(ks_pool[r:P:32, :].bitcast(I32), k_scales[0, r:16:4, :].bitcast(I32))
-        warm = held.tile([P, 1], F32, name="warm")
-        nc.scalar.activation(warm[0:64, :], vs_pool[0:64, 0:1], ACT.Exp)
-        for r in range(4):
-            nc.scalar.dma_start(q_plane[r:P:32, :].bitcast(I32), q_scales[0, 0, r:16:4, :].bitcast(I32))
+            nc.sync.dma_start(q_plane[r:P:32, :].bitcast(I32), q_scales[0, 0, r:16:4, :].bitcast(I32))
+        v_pool = held.tile([P, T], F32, name="v_pool", tag="v_pool", align_bytes=64)
+        load_pool(v_pool, vT)
 
         ident = held.tile([P, P], F32, name="ident", align_bytes=64)
         make_identity(nc, ident[:])
 
-        vs_slot = []
-        for g in range(PASSES):
-            vs_row = held.tile([P, PASS], F32, name="vs_row%d" % g, align_bytes=64)
+        def token_scales(g, tag, bank):
+            vs_row = held.tile([P, PASS], F32, name="vs_row%d" % g, tag=tag, align_bytes=64)
             nc.vector.tensor_copy(vs_row[:], vs_pool[:].indirect(slots(g)))
-            vs_turned = psum.tile([P, PACK, P], F32, name="vs_turned%d" % g, tag="turn%d" % g)
+            vs_turned = psum.tile([P, PACK, P], F32, name="vs_turned%d" % g, tag=bank)
             for t in range(PACK):
                 nc.tensor.transpose(vs_turned[:, t, :], vs_row[:, t:PASS:PACK], ident[:])
             col = held.tile([P, PACK], F32, name="vs_slot%d" % g)
             nc.scalar.copy(col[:], vs_turned[:, :, P - 1])
-            vs_slot.append(col)
+            return col
+
+        vs_slot = [token_scales(0, "vs_row", "turn0")]
 
         k_plane = held.tile([P, N], U8, name="k_plane", align_bytes=64)
         nc.vector.tensor_copy(k_plane[:], ks_pool[:].indirect(offsets[:]))
@@ -90,7 +94,7 @@ def tile_attend_qpk_cap_srt_kernel(tc, q_words, q_scales, k_words, k_scales, vT,
         for g in range(PASSES):
             k_codes = k_listed[:, g * PASS : (g + 1) * PASS]
             nc.vector.tensor_copy(k_codes.bitcast(U32), k_pool[:, 0 : reach(g)].bitcast(U32).indirect(slots(g)))
-            score = psum.tile([P, PASS], F32, name="score%d" % g)
+            score = psum.tile([P, PASS], F32, name="score%d" % g, tag="score%d" % g)
             nc.tensor.matmul_mx(
                 out=score[:],
                 lhsT=q_codes[:].bitcast(FP8X4),
@@ -103,6 +107,8 @@ def tile_attend_qpk_cap_srt_kernel(tc, q_words, q_scales, k_words, k_scales, vT,
             th = held.tile([P, PACK, P], F32, name="tanh%d" % g, tag="tanh%d" % g, align_bytes=64)
             nc.scalar.activation(th[:], score[:].rearrange("q (s t) -> q t s", t=PACK), ACT.Tanh, scale=1.0 / CAP)
             tanh_half.append(th)
+
+        vs_slot.append(token_scales(1, "k_pool", "score0"))
 
         neg_c = []
         neg_m = None

@@ -45,31 +45,34 @@ def tile_attend_qpk_cap_srt_kernel(tc, q_words, q_scales, k_words, k_scales, vT,
 
         ks_pool = held.tile([P, T], U8, name="ks_pool", tag="ks_pool", align_bytes=64)
         nc.gpsimd.memset(ks_pool[:].bitcast(I32), 0)
-        q_plane = held.tile([P, NQ], U8, name="q_plane", align_bytes=64)
-        nc.gpsimd.memset(q_plane[:].bitcast(I32), 0)
         vs_pool = held.tile([P, T], F32, name="vs_pool", align_bytes=64)
         nc.vector.memset(vs_pool[0 : P - 1, 0:63], 0.0)
-        nc.vector.memset(vs_pool[0 : P - 1, 63:2368], 0.0)
-        nc.gpsimd.memset(vs_pool[0 : P - 1, 2368:T], 0.0)
+        nc.vector.memset(vs_pool[0 : P - 1, 63:2496], 0.0)
+        nc.gpsimd.memset(vs_pool[0 : P - 1, 2496:T], 0.0)
+        q_plane = held.tile([P, NQ], U8, name="q_plane", align_bytes=64)
+        nc.gpsimd.memset(q_plane[:].bitcast(I32), 0)
 
         warm = held.tile([P, 1], F32, name="warm")
         nc.scalar.activation(warm[0:64, :], vs_pool[0:64, 0:1], ACT.Exp)
 
-        def load_pool(pool_tile, source):
-            nc.sync.dma_start(pool_tile[:, 0 : reach(0)], source[:, 0 : reach(0)])
-            nc.sync.dma_start(pool_tile[:, reach(0) : T], source[:, reach(0) : T])
+        def load_columns(pool_tile, source, lo, hi):
+            nc.sync.dma_start(pool_tile[:, lo:hi], source[:, lo:hi])
 
+        k_pool = held.tile([P, T], I32, name="k_pool", tag="k_pool", align_bytes=64)
+        k_source = k_words[0].rearrange("p n t -> p (n t)").bitcast(I32)
         nc.sync.dma_start(vs_pool[P - 1 : P, :], vs[0:1, :])
+        load_columns(k_pool, k_source, 0, 512)
         for r in range(4):
             nc.sync.dma_start(ks_pool[r:P:32, :].bitcast(I32), k_scales[0, r:16:4, :].bitcast(I32))
-        k_pool = held.tile([P, T], I32, name="k_pool", tag="k_pool", align_bytes=64)
-        load_pool(k_pool, k_words[0].rearrange("p n t -> p (n t)").bitcast(I32))
+        load_columns(k_pool, k_source, 512, reach(0))
+        load_columns(k_pool, k_source, reach(0), T)
         q_codes = held.tile([P, NQ], I32, name="q_codes", align_bytes=64)
         nc.sync.dma_start(q_codes[:], q_words[0, 0].rearrange("p n t -> p (n t)").bitcast(I32))
         for r in range(4):
             nc.sync.dma_start(q_plane[r:P:32, :].bitcast(I32), q_scales[0, 0, r:16:4, :].bitcast(I32))
         v_pool = held.tile([P, T], F32, name="v_pool", tag="v_pool", align_bytes=64)
-        load_pool(v_pool, vT)
+        load_columns(v_pool, vT, 0, reach(0))
+        load_columns(v_pool, vT, reach(0), T)
 
         ident = held.tile([P, P], F32, name="ident", align_bytes=64)
         make_identity(nc, ident[:])

@@ -35,7 +35,6 @@ def tile_attend_qpk_cap_srt_kernel(tc, q_words, q_scales, k_words, k_scales, vT,
         psum = ctx.enter_context(tc.psum_pool(name="psum", bufs=1))
 
         offsets = held.tile([P, N // 16], U16, name="offsets")
-        nc.sync.dma_start(offsets[:], offs)
 
         def reach(g):
             return T - (N - (g + 1) * PASS)
@@ -60,8 +59,9 @@ def tile_attend_qpk_cap_srt_kernel(tc, q_words, q_scales, k_words, k_scales, vT,
 
         k_pool = held.tile([P, T], I32, name="k_pool", tag="k_pool", align_bytes=64)
         k_source = k_words[0].rearrange("p n t -> p (n t)").bitcast(I32)
-        nc.sync.dma_start(vs_pool[P - 1 : P, :], vs[0:1, :])
         load_columns(k_pool, k_source, 0, 512)
+        nc.sync.dma_start(offsets[:], offs)
+        nc.sync.dma_start(vs_pool[P - 1 : P, :], vs[0:1, :])
         for r in range(4):
             nc.sync.dma_start(ks_pool[r:P:32, :].bitcast(I32), k_scales[0, r:16:4, :].bitcast(I32))
         load_columns(k_pool, k_source, 512, reach(0))
@@ -77,17 +77,29 @@ def tile_attend_qpk_cap_srt_kernel(tc, q_words, q_scales, k_words, k_scales, vT,
         ident = held.tile([P, P], F32, name="ident", align_bytes=64)
         make_identity(nc, ident[:])
 
-        def token_scales(g, tag, bank):
+        def by_place(listed, u):
+            return listed.rearrange("r (b u j h) -> r u h b j", u=2, j=8, h=2)[:, u]
+
+        def place_pair(placed, u):
+            return placed[:, 2 * u : 2 * u + 2, :].rearrange("r h (b j) -> r h b j", j=8)
+
+        def gather_scales(g, tag):
             vs_row = held.tile([P, PASS], F32, name="vs_row%d" % g, tag=tag, align_bytes=64)
             nc.vector.tensor_copy(vs_row[:], vs_pool[:].indirect(slots(g)))
+            return vs_row
+
+        def turn_scales(g, vs_row, tag, bank):
+            vs_placed = held.tile([P, PACK, P], F32, name="vs_placed%d" % g, tag=tag, align_bytes=64)
+            for u in range(2):
+                nc.scalar.copy(place_pair(vs_placed, u), by_place(vs_row[:], u))
             vs_turned = psum.tile([P, PACK, P], F32, name="vs_turned%d" % g, tag=bank)
             for t in range(PACK):
-                nc.tensor.transpose(vs_turned[:, t, :], vs_row[:, t:PASS:PACK], ident[:])
+                nc.tensor.transpose(vs_turned[:, t, :], vs_placed[:, t, :], ident[:])
             col = held.tile([P, PACK], F32, name="vs_slot%d" % g)
             nc.scalar.copy(col[:], vs_turned[:, :, P - 1])
             return col
 
-        vs_slot = [token_scales(0, "vs_row", "turn0")]
+        vs_slot = [turn_scales(0, gather_scales(0, "vs_row"), "vs_placed", "turn0")]
 
         k_plane = held.tile([P, N], U8, name="k_plane", align_bytes=64)
         nc.vector.tensor_copy(k_plane[:], ks_pool[:].indirect(offsets[:]))
@@ -108,10 +120,11 @@ def tile_attend_qpk_cap_srt_kernel(tc, q_words, q_scales, k_words, k_scales, vT,
                 stop=True,
             )
             th = held.tile([P, PACK, P], F32, name="tanh%d" % g, tag="tanh%d" % g, align_bytes=64)
-            nc.scalar.activation(th[:], score[:].rearrange("q (s t) -> q t s", t=PACK), ACT.Tanh, scale=1.0 / CAP)
+            for u in range(2):
+                nc.scalar.activation(place_pair(th, u), by_place(score[:], u), ACT.Tanh, scale=1.0 / CAP)
             tanh_half.append(th)
 
-        vs_slot.append(token_scales(1, "k_pool", "score0"))
+        late_row = gather_scales(1, "k_pool")
 
         neg_c = []
         neg_m = None
@@ -123,6 +136,8 @@ def tile_attend_qpk_cap_srt_kernel(tc, q_words, q_scales, k_words, k_scales, vT,
             )
             neg_m = least[:]
             neg_c.append(nc_g)
+
+        vs_slot.append(turn_scales(1, late_row, "tanh0", "score0"))
 
         turned = []
         sums = []
@@ -143,7 +158,7 @@ def tile_attend_qpk_cap_srt_kernel(tc, q_words, q_scales, k_words, k_scales, vT,
         for g in range(PASSES):
             v_pairs = v_all[:, g * PASS : (g + 1) * PASS]
             nc.vector.tensor_copy(
-                v_pairs.rearrange("e (u s h) -> e s u h", u=2, h=2), v_pool[:, 0 : reach(g)].indirect(slots(g))
+                v_pairs.rearrange("e (u b x) -> e b u x", u=2, x=16), v_pool[:, 0 : reach(g)].indirect(slots(g))
             )
             bank = psum.tile([P, 2, P], F32, name="v_turned%d" % g)
             for u in range(2):

@@ -104,10 +104,9 @@ def tile_attend_qpk_cap_srt_kernel(tc, q_words, q_scales, k_words, k_scales, vT,
         k_plane = held.tile([P, N], U8, name="k_plane", align_bytes=64)
         nc.vector.tensor_copy(k_plane[:], ks_pool[:].indirect(offsets[:]))
 
-        k_listed = held.tile([P, N], I32, name="k_listed", tag="ks_pool", align_bytes=64)
-        tanh_half = []
+        tanh_all = held.tile([P, PASSES, PACK, P], F32, name="tanh_all", align_bytes=64)
         for g in range(PASSES):
-            k_codes = k_listed[:, g * PASS : (g + 1) * PASS]
+            k_codes = held.tile([P, PASS], I32, name="k_listed%d" % g, tag="listed%d" % g, align_bytes=64)[:]
             nc.vector.tensor_copy(k_codes.bitcast(U32), k_pool[:, 0 : reach(g)].bitcast(U32).indirect(slots(g)))
             score = psum.tile([P, PASS], F32, name="score%d" % g, tag="score%d" % g)
             nc.tensor.matmul_mx(
@@ -119,44 +118,46 @@ def tile_attend_qpk_cap_srt_kernel(tc, q_words, q_scales, k_words, k_scales, vT,
                 start=True,
                 stop=True,
             )
-            th = held.tile([P, PACK, P], F32, name="tanh%d" % g, tag="tanh%d" % g, align_bytes=64)
             for u in range(2):
-                nc.scalar.activation(place_pair(th, u), by_place(score[:], u), ACT.Tanh, scale=1.0 / CAP)
-            tanh_half.append(th)
+                nc.scalar.activation(place_pair(tanh_all[:, g], u), by_place(score[:], u), ACT.Tanh, scale=1.0 / CAP)
 
-        late_row = gather_scales(1, "k_pool")
+        late_row = gather_scales(1, "listed0")
 
-        neg_c = []
-        neg_m = None
+        neg_c = held.tile([P, N], F32, name="neg_c", align_bytes=64)
+        least = [held.tile([P, 1], F32, name="least%d" % g) for g in range(PASSES)]
         for g in range(PASSES):
-            nc_g = held.tile([P, PASS], F32, name="neg_c%d" % g, align_bytes=64)
-            least = held.tile([P, 1], F32, name="neg_m%d" % g)
             nc.vector.tensor_scalar(
-                nc_g[:], tanh_half[g][:].rearrange("q t s -> q (t s)"), -CAP, neg_m, ALU.mult, ALU.min, accum_out=least[:]
+                neg_c[:, g * PASS : (g + 1) * PASS],
+                tanh_all[:, g].rearrange("q t s -> q (t s)"),
+                -CAP,
+                least[g - 1][:] if g else None,
+                ALU.mult,
+                ALU.min,
+                accum_out=least[g][:],
             )
-            neg_m = least[:]
-            neg_c.append(nc_g)
+        neg_m = least[PASSES - 1][:]
 
-        vs_slot.append(turn_scales(1, late_row, "tanh0", "score0"))
+        vs_slot.append(turn_scales(1, late_row, "listed1", "score0"))
 
         turned = []
-        sums = []
+        sums = held.tile([P, 2 * PASSES], F32, name="sums")
         for g in range(PASSES):
-            p = held.tile([P, PASS], F32, name="p%d" % g, align_bytes=64)
-            total = held.tile([P, 1], F32, name="sum%d" % g)
-            nc.scalar.activation(p[:], neg_c[g][:], ACT.Exp, bias=neg_m, scale=-1.0, accum_out=total[:])
-            sums.append(total)
             p_turned = psum.tile([P, PACK, P], F32, name="p_turned%d" % g, tag="turn%d" % g)
-            for t in range(PACK):
-                nc.tensor.transpose(p_turned[:, t, :], p[:, t * P : (t + 1) * P], ident[:])
+            for u in range(2):
+                p = held.tile([P, 2 * P], F32, name="p%d%d" % (g, u), align_bytes=64)
+                lo = g * PASS + u * 2 * P
+                nc.scalar.activation(
+                    p[:], neg_c[:, lo : lo + 2 * P], ACT.Exp, bias=neg_m, scale=-1.0, accum_out=sums[:, 2 * g + u : 2 * g + u + 1]
+                )
+                for h in range(2):
+                    nc.tensor.transpose(p_turned[:, 2 * u + h, :], p[:, h * P : (h + 1) * P], ident[:])
             turned.append(p_turned)
         row_sum = held.tile([P, 1], F32, name="row_sum")
-        nc.scalar.activation(row_sum[:], sums[0][:], ACT.Identity, bias=sums[1][:], scale=1.0)
+        nc.scalar.activation(sums[:], sums[:], ACT.Identity, accum_out=row_sum[:])
 
-        v_all = held.tile([P, N], BF16, name="v_all", tag="tanh%d" % (PASSES - 1), align_bytes=64)
         v_turned = []
         for g in range(PASSES):
-            v_pairs = v_all[:, g * PASS : (g + 1) * PASS]
+            v_pairs = held.tile([P, PASS], BF16, name="v_pairs%d" % g, tag=("listed0", "v_pairs1")[g], align_bytes=64)[:]
             nc.vector.tensor_copy(
                 v_pairs.rearrange("e (u b x) -> e b u x", u=2, x=16), v_pool[:, 0 : reach(g)].indirect(slots(g))
             )

@@ -42,14 +42,18 @@ def tile_attend_qpk_cap_srt_kernel(tc, q_words, q_scales, k_words, k_scales, vT,
         def slots(g):
             return offsets[:, g * LIST_COLS : (g + 1) * LIST_COLS]
 
-        ks_pool = held.tile([P, T], U8, name="ks_pool", tag="ks_pool", align_bytes=64)
+        planes = held.tile([P, N + NQ], U8, name="planes", align_bytes=64)
+        nc.vector.memset(planes[:].bitcast(I32)[:, 0:145], 0)
+        nc.vector.memset(planes[:].bitcast(I32)[:, 145 : (N + NQ) // 4], 0)
+        k_plane = planes[:, 0:N]
+        q_plane = planes[:, N : N + NQ]
+        ks_pool = held.tile([P, T], U8, name="ks_pool", align_bytes=64)
         nc.gpsimd.memset(ks_pool[:].bitcast(I32), 0)
         vs_pool = held.tile([P, T], F32, name="vs_pool", align_bytes=64)
         nc.vector.memset(vs_pool[0 : P - 1, 0:63], 0.0)
-        nc.vector.memset(vs_pool[0 : P - 1, 63:2496], 0.0)
-        nc.gpsimd.memset(vs_pool[0 : P - 1, 2496:T], 0.0)
-        q_plane = held.tile([P, NQ], U8, name="q_plane", align_bytes=64)
-        nc.gpsimd.memset(q_plane[:].bitcast(I32), 0)
+        nc.vector.memset(vs_pool[0 : P - 1, 63:1920], 0.0)
+        nc.gpsimd.memset(vs_pool[0 : P - 1, 1920 : reach(0)], 0.0)
+        nc.gpsimd.memset(vs_pool[0 : P - 1, reach(0) : T], 0.0)
 
         warm = held.tile([P, 1], F32, name="warm")
         nc.scalar.activation(warm[0:64, :], vs_pool[0:64, 0:1], ACT.Exp)
@@ -59,20 +63,20 @@ def tile_attend_qpk_cap_srt_kernel(tc, q_words, q_scales, k_words, k_scales, vT,
 
         k_pool = held.tile([P, T], I32, name="k_pool", tag="k_pool", align_bytes=64)
         k_source = k_words[0].rearrange("p n t -> p (n t)").bitcast(I32)
-        load_columns(k_pool, k_source, 0, 512)
         nc.sync.dma_start(offsets[:], offs)
-        nc.sync.dma_start(vs_pool[P - 1 : P, :], vs[0:1, :])
-        for r in range(4):
-            nc.sync.dma_start(ks_pool[r:P:32, :].bitcast(I32), k_scales[0, r:16:4, :].bitcast(I32))
-        load_columns(k_pool, k_source, 512, reach(0))
-        load_columns(k_pool, k_source, reach(0), T)
         q_codes = held.tile([P, NQ], I32, name="q_codes", align_bytes=64)
         nc.sync.dma_start(q_codes[:], q_words[0, 0].rearrange("p n t -> p (n t)").bitcast(I32))
+        load_columns(k_pool, k_source, 0, 960)
+        nc.sync.dma_start(ks_pool[0:P:8, :].bitcast(I32), k_scales[0].bitcast(I32))
+        load_columns(k_pool, k_source, 960, 2304)
         for r in range(4):
-            nc.sync.dma_start(q_plane[r:P:32, :].bitcast(I32), q_scales[0, 0, r:16:4, :].bitcast(I32))
+            nc.sync.dma_start(planes[r:P:32, N : N + NQ].bitcast(I32), q_scales[0, 0, r:16:4, :].bitcast(I32))
+        nc.sync.dma_start(vs_pool[P - 1 : P, 0 : reach(0)], vs[0:1, 0 : reach(0)])
+        load_columns(k_pool, k_source, 2304, reach(0))
+        load_columns(k_pool, k_source, reach(0), T)
+        nc.sync.dma_start(vs_pool[P - 1 : P, reach(0) : T], vs[0:1, reach(0) : T])
         v_pool = held.tile([P, T], F32, name="v_pool", tag="v_pool", align_bytes=64)
-        load_columns(v_pool, vT, 0, reach(0))
-        load_columns(v_pool, vT, reach(0), T)
+        load_columns(v_pool, vT, 0, 512)
 
         ident = held.tile([P, P], F32, name="ident", align_bytes=64)
         make_identity(nc, ident[:])
@@ -85,7 +89,7 @@ def tile_attend_qpk_cap_srt_kernel(tc, q_words, q_scales, k_words, k_scales, vT,
 
         def gather_scales(g, tag):
             vs_row = held.tile([P, PASS], F32, name="vs_row%d" % g, tag=tag, align_bytes=64)
-            nc.vector.tensor_copy(vs_row[:], vs_pool[:].indirect(slots(g)))
+            nc.vector.tensor_copy(vs_row[:], vs_pool[:, 0 : reach(g)].indirect(slots(g)))
             return vs_row
 
         def turn_scales(g, vs_row, tag, bank):
@@ -95,33 +99,42 @@ def tile_attend_qpk_cap_srt_kernel(tc, q_words, q_scales, k_words, k_scales, vT,
             vs_turned = psum.tile([P, PACK, P], F32, name="vs_turned%d" % g, tag=bank)
             for t in range(PACK):
                 nc.tensor.transpose(vs_turned[:, t, :], vs_placed[:, t, :], ident[:])
-            col = held.tile([P, PACK], F32, name="vs_slot%d" % g)
+            col = held.tile([P, PACK], F32, name="vs_slot%d" % g, tag="vs_slot%d" % g, align_bytes=64)
             nc.scalar.copy(col[:], vs_turned[:, :, P - 1])
             return col
 
-        vs_slot = [turn_scales(0, gather_scales(0, "vs_row"), "vs_placed", "turn0")]
+        ks_listed = held.tile([P, N], U8, name="ks_listed", align_bytes=64)
+        nc.vector.tensor_copy(ks_listed[:], ks_pool[:].indirect(offsets[:]))
+        for r in range(4):
+            nc.sync.dma_start(planes[r:P:32, 0:N].bitcast(I32), ks_listed[8 * r : P : 32, :].bitcast(I32))
+        load_columns(v_pool, vT, 512, reach(0))
+        load_columns(v_pool, vT, reach(0), T)
 
-        k_plane = held.tile([P, N], U8, name="k_plane", align_bytes=64)
-        nc.vector.tensor_copy(k_plane[:], ks_pool[:].indirect(offsets[:]))
+        early_row = gather_scales(0, "vs_row")
 
         tanh_all = held.tile([P, PASSES, PACK, P], F32, name="tanh_all", align_bytes=64)
         for g in range(PASSES):
             k_codes = held.tile([P, PASS], I32, name="k_listed%d" % g, tag="listed%d" % g, align_bytes=64)[:]
             nc.vector.tensor_copy(k_codes.bitcast(U32), k_pool[:, 0 : reach(g)].bitcast(U32).indirect(slots(g)))
-            score = psum.tile([P, PASS], F32, name="score%d" % g, tag="score%d" % g)
-            nc.tensor.matmul_mx(
-                out=score[:],
-                lhsT=q_codes[:].bitcast(FP8X4),
-                lhsT_scale=q_plane[:],
-                rhs=k_codes.bitcast(FP8X4),
-                rhs_scale=k_plane[:, g * PASS : (g + 1) * PASS],
-                start=True,
-                stop=True,
-            )
-            for u in range(2):
-                nc.scalar.activation(place_pair(tanh_all[:, g], u), by_place(score[:], u), ACT.Tanh, scale=1.0 / CAP)
+            pieces = g + 1
+            width = PASS // pieces
+            for c in range(pieces):
+                score = psum.tile([P, width], F32, name="score%d%d" % (g, c), tag="score%d%d" % (g, c))
+                nc.tensor.matmul_mx(
+                    out=score[:],
+                    lhsT=q_codes[:].bitcast(FP8X4),
+                    lhsT_scale=q_plane,
+                    rhs=k_codes[:, c * width : (c + 1) * width].bitcast(FP8X4),
+                    rhs_scale=k_plane[:, g * PASS + c * width : g * PASS + (c + 1) * width],
+                    start=True,
+                    stop=True,
+                )
+                for u in range(2):
+                    rows = tanh_all[:, g, :, c * width // PACK : (c + 1) * width // PACK]
+                    nc.scalar.activation(place_pair(rows, u), by_place(score[:], u), ACT.Tanh, scale=1.0 / CAP)
 
-        late_row = gather_scales(1, "listed0")
+        vs_slot = [turn_scales(0, early_row, "vs_placed", "score00")]
+        late_row = gather_scales(1, "late_row")
 
         neg_c = held.tile([P, N], F32, name="neg_c", align_bytes=64)
         least = [held.tile([P, 1], F32, name="least%d" % g) for g in range(PASSES)]
@@ -137,7 +150,7 @@ def tile_attend_qpk_cap_srt_kernel(tc, q_words, q_scales, k_words, k_scales, vT,
             )
         neg_m = least[PASSES - 1][:]
 
-        vs_slot.append(turn_scales(1, late_row, "listed1", "score0"))
+        vs_slot.append(turn_scales(1, late_row, "listed1", "turn1"))
 
         turned = []
         sums = held.tile([P, 2 * PASSES], F32, name="sums")
@@ -157,7 +170,7 @@ def tile_attend_qpk_cap_srt_kernel(tc, q_words, q_scales, k_words, k_scales, vT,
 
         v_turned = []
         for g in range(PASSES):
-            v_pairs = held.tile([P, PASS], BF16, name="v_pairs%d" % g, tag=("listed0", "v_pairs1")[g], align_bytes=64)[:]
+            v_pairs = held.tile([P, PASS], BF16, name="v_pairs%d" % g, tag=("late_row", "v_pairs1")[g], align_bytes=64)[:]
             nc.vector.tensor_copy(
                 v_pairs.rearrange("e (u b x) -> e b u x", u=2, x=16), v_pool[:, 0 : reach(g)].indirect(slots(g))
             )
@@ -166,33 +179,42 @@ def tile_attend_qpk_cap_srt_kernel(tc, q_words, q_scales, k_words, k_scales, vT,
                 nc.tensor.transpose(bank[:, u, :], v_pairs.bitcast(F32)[:, u * P : (u + 1) * P], ident[:])
             v_turned.append(bank)
 
-        late = held.tile([P, 2 * N + 2], BF16, name="late", tag="v_pool", align_bytes=64)
-        wv = [late[:, 2 * PASS * g : 2 * PASS * (g + 1)] for g in range(PASSES)]
-        inv_sum = late[:, 2 * N : 2 * N + 2].bitcast(F32)
+        late = held.tile([P, N + 2], BF16, name="late", tag="v_pool", align_bytes=64)
+        inv_sum = late[:, N : N + 2].bitcast(F32)
+        v_grouped = []
         for g in range(PASSES):
+            grouped = held.tile([P, PASS], BF16, name="v_grouped%d" % g, align_bytes=64)
             nc.scalar.copy(
-                wv[g][:, PASS : 2 * PASS].bitcast(F32).rearrange("s (e u) -> s e u", u=2),
-                v_turned[g][:].rearrange("s u e -> s e u"),
+                grouped[:].bitcast(F32).rearrange("s (e u) -> s e u", u=2), v_turned[g][:].rearrange("s u e -> s e u")
             )
+            v_grouped.append(grouped)
             nc.vector.tensor_tensor(
-                wv[g][:, 0:PASS].rearrange("s (q t) -> s q t", t=PACK),
+                late[:, g * PASS : (g + 1) * PASS].rearrange("s (q t) -> s q t", t=PACK),
                 turned[g][:].rearrange("s t q -> s q t"),
                 vs_slot[g][:].unsqueeze(1).to_broadcast([P, NQ, PACK]),
                 ALU.mult,
             )
         nc.vector.reciprocal(inv_sum, row_sum[:])
 
+        w_codes = held.tile([P, PASSES, NQ], U32, name="w_codes", align_bytes=64)
+        v_codes = held.tile([P, PASSES, DV], U32, name="v_codes", tag="vs_slot0", align_bytes=64)
+        w_plane = held.tile([P, PASSES, NQ], U8, name="w_plane", align_bytes=64)
+        v_plane = held.tile([P, PASSES, DV], U8, name="v_plane", align_bytes=64)
+        for g in range(PASSES):
+            nc.vector.quantize_mx(
+                out=w_codes[:, g, :].bitcast(FP8X4), scales=w_plane[:, g, :], in_=late[:, g * PASS : (g + 1) * PASS]
+            )
+        for g in range(PASSES):
+            nc.vector.quantize_mx(out=v_codes[:, g, :].bitcast(FP8X4), scales=v_plane[:, g, :], in_=v_grouped[g][:])
+
         acc = psum.tile([P, DV], F32, name="acc")
         for g in range(PASSES):
-            codes = held.tile([P, 2 * P], U32, name="codes%d" % g, align_bytes=64)
-            plane = held.tile([P, 2 * P], U8, name="plane%d" % g, align_bytes=64)
-            nc.vector.quantize_mx(out=codes[:].bitcast(FP8X4), scales=plane[:], in_=wv[g])
             nc.tensor.matmul_mx(
                 out=acc[:],
-                lhsT=codes[:, 0:P].bitcast(FP8X4),
-                lhsT_scale=plane[:, 0:P],
-                rhs=codes[:, P : 2 * P].bitcast(FP8X4),
-                rhs_scale=plane[:, P : 2 * P],
+                lhsT=w_codes[:, g, :].bitcast(FP8X4),
+                lhsT_scale=w_plane[:, g, :],
+                rhs=v_codes[:, g, :].bitcast(FP8X4),
+                rhs_scale=v_plane[:, g, :],
                 start=(g == 0),
                 stop=(g == PASSES - 1),
             )

@@ -55,26 +55,27 @@ def tile_attend_qpk_cap_srt_kernel(tc, q_words, q_scales, k_words, k_scales, vT,
         nc.gpsimd.memset(vs_pool[0 : P - 1, 1920 : reach(0)], 0.0)
         nc.gpsimd.memset(vs_pool[0 : P - 1, reach(0) : T], 0.0)
 
-        warm = held.tile([P, 1], F32, name="warm")
-        nc.scalar.activation(warm[0:64, :], vs_pool[0:64, 0:1], ACT.Exp)
-
         def load_columns(pool_tile, source, lo, hi):
             nc.sync.dma_start(pool_tile[:, lo:hi], source[:, lo:hi])
 
         k_pool = held.tile([P, T], I32, name="k_pool", tag="k_pool", align_bytes=64)
         k_source = k_words[0].rearrange("p n t -> p (n t)").bitcast(I32)
+        def load_query_scales(r):
+            nc.sync.dma_start(planes[r:P:32, N : N + NQ].bitcast(I32), q_scales[0, 0, r:16:4, :].bitcast(I32))
+
+        load_columns(k_pool, k_source, 0, 1152)
         nc.sync.dma_start(offsets[:], offs)
+        nc.sync.dma_start(ks_pool[0:P:8, :].bitcast(I32), k_scales[0].bitcast(I32))
+        nc.sync.dma_start(vs_pool[P - 1 : P, :], vs[0:1, :])
         q_codes = held.tile([P, NQ], I32, name="q_codes", align_bytes=64)
         nc.sync.dma_start(q_codes[:], q_words[0, 0].rearrange("p n t -> p (n t)").bitcast(I32))
-        load_columns(k_pool, k_source, 0, 960)
-        nc.sync.dma_start(ks_pool[0:P:8, :].bitcast(I32), k_scales[0].bitcast(I32))
-        load_columns(k_pool, k_source, 960, 2304)
-        for r in range(4):
-            nc.sync.dma_start(planes[r:P:32, N : N + NQ].bitcast(I32), q_scales[0, 0, r:16:4, :].bitcast(I32))
-        nc.sync.dma_start(vs_pool[P - 1 : P, 0 : reach(0)], vs[0:1, 0 : reach(0)])
-        load_columns(k_pool, k_source, 2304, reach(0))
+        load_query_scales(0)
+        load_query_scales(1)
+        load_columns(k_pool, k_source, 1152, 2880)
+        load_query_scales(2)
+        load_query_scales(3)
+        load_columns(k_pool, k_source, 2880, reach(0))
         load_columns(k_pool, k_source, reach(0), T)
-        nc.sync.dma_start(vs_pool[P - 1 : P, reach(0) : T], vs[0:1, reach(0) : T])
         v_pool = held.tile([P, T], F32, name="v_pool", tag="v_pool", align_bytes=64)
         load_columns(v_pool, vT, 0, 512)
 
@@ -134,7 +135,7 @@ def tile_attend_qpk_cap_srt_kernel(tc, q_words, q_scales, k_words, k_scales, vT,
                     nc.scalar.activation(place_pair(rows, u), by_place(score[:], u), ACT.Tanh, scale=1.0 / CAP)
 
         vs_slot = [turn_scales(0, early_row, "vs_placed", "score00")]
-        late_row = gather_scales(1, "late_row")
+        late_row = gather_scales(1, "k_pool")
 
         neg_c = held.tile([P, N], F32, name="neg_c", align_bytes=64)
         least = [held.tile([P, 1], F32, name="least%d" % g) for g in range(PASSES)]
@@ -170,7 +171,7 @@ def tile_attend_qpk_cap_srt_kernel(tc, q_words, q_scales, k_words, k_scales, vT,
 
         v_turned = []
         for g in range(PASSES):
-            v_pairs = held.tile([P, PASS], BF16, name="v_pairs%d" % g, tag=("late_row", "v_pairs1")[g], align_bytes=64)[:]
+            v_pairs = held.tile([P, PASS], BF16, name="v_pairs%d" % g, tag=("k_pool", "v_pairs1")[g], align_bytes=64)[:]
             nc.vector.tensor_copy(
                 v_pairs.rearrange("e (u b x) -> e b u x", u=2, x=16), v_pool[:, 0 : reach(g)].indirect(slots(g))
             )

@@ -42,51 +42,46 @@ def tile_attend_qpk_cap_srt_kernel(tc, q_words, q_scales, k_words, k_scales, vT,
         def slots(g):
             return offsets[:, g * LIST_COLS : (g + 1) * LIST_COLS]
 
-        planes = held.tile([P, N + NQ], U8, name="planes", align_bytes=64)
-        nc.vector.memset(planes[:].bitcast(I32)[:, 0:145], 0)
-        nc.vector.memset(planes[:].bitcast(I32)[:, 145 : (N + NQ) // 4], 0)
+        ks_pool = held.tile([P, T + 4], U8, name="ks_pool", align_bytes=64)
+        planes = held.tile([P, N + NQ + 4], U8, name="planes", align_bytes=64)
+        vs_pool = held.tile([P, T], F32, name="vs_pool", align_bytes=64)
+        nc.vector.memset(planes[:].bitcast(I32), 0)
+        nc.vector.memset(ks_pool[0:48, :].bitcast(I32), 0)
+        nc.gpsimd.memset(ks_pool[64:P, 0:T].bitcast(I32), 0)
+        nc.vector.memset(vs_pool[0 : P - 1, 0:1], 0.0)
+        nc.vector.memset(vs_pool[0 : P - 1, 1:704], 0.0)
+        nc.gpsimd.memset(vs_pool[0 : P - 1, 704 : reach(0)], 0.0)
+        nc.gpsimd.memset(vs_pool[0 : P - 1, reach(0) : T], 0.0)
         k_plane = planes[:, 0:N]
         q_plane = planes[:, N : N + NQ]
-        ks_pool = held.tile([P, T], U8, name="ks_pool", align_bytes=64)
-        nc.gpsimd.memset(ks_pool[:].bitcast(I32), 0)
-        vs_pool = held.tile([P, T], F32, name="vs_pool", align_bytes=64)
-        nc.vector.memset(vs_pool[0 : P - 1, 0:63], 0.0)
-        nc.vector.memset(vs_pool[0 : P - 1, 63:1920], 0.0)
-        nc.gpsimd.memset(vs_pool[0 : P - 1, 1920 : reach(0)], 0.0)
-        nc.gpsimd.memset(vs_pool[0 : P - 1, reach(0) : T], 0.0)
 
         def load_columns(pool_tile, source, lo, hi):
             nc.sync.dma_start(pool_tile[:, lo:hi], source[:, lo:hi])
 
         k_pool = held.tile([P, T], I32, name="k_pool", tag="k_pool", align_bytes=64)
         k_source = k_words[0].rearrange("p n t -> p (n t)").bitcast(I32)
+
         def load_query_scales(r):
             nc.sync.dma_start(planes[r:P:32, N : N + NQ].bitcast(I32), q_scales[0, 0, r:16:4, :].bitcast(I32))
 
-        load_columns(k_pool, k_source, 0, 1152)
+        nc.sync.dma_start(ks_pool[48:64, 0:T].bitcast(I32), k_scales[0].bitcast(I32))
         nc.sync.dma_start(offsets[:], offs)
-        nc.sync.dma_start(ks_pool[0:P:8, :].bitcast(I32), k_scales[0].bitcast(I32))
+        load_columns(k_pool, k_source, 0, 1536)
         nc.sync.dma_start(vs_pool[P - 1 : P, :], vs[0:1, :])
         q_codes = held.tile([P, NQ], I32, name="q_codes", align_bytes=64)
         nc.sync.dma_start(q_codes[:], q_words[0, 0].rearrange("p n t -> p (n t)").bitcast(I32))
-        load_query_scales(0)
-        load_query_scales(1)
-        load_columns(k_pool, k_source, 1152, 2880)
-        load_query_scales(2)
-        load_query_scales(3)
-        load_columns(k_pool, k_source, 2880, reach(0))
+        for r in range(3):
+            load_query_scales(r)
+        load_columns(k_pool, k_source, 1536, reach(0))
         load_columns(k_pool, k_source, reach(0), T)
+        load_query_scales(3)
         v_pool = held.tile([P, T], F32, name="v_pool", tag="v_pool", align_bytes=64)
-        load_columns(v_pool, vT, 0, 512)
 
         ident = held.tile([P, P], F32, name="ident", align_bytes=64)
         make_identity(nc, ident[:])
 
         def by_place(listed, u):
             return listed.rearrange("r (b u j h) -> r u h b j", u=2, j=8, h=2)[:, u]
-
-        def place_pair(placed, u):
-            return placed[:, 2 * u : 2 * u + 2, :].rearrange("r h (b j) -> r h b j", j=8)
 
         def gather_scales(g, tag):
             vs_row = held.tile([P, PASS], F32, name="vs_row%d" % g, tag=tag, align_bytes=64)
@@ -95,8 +90,10 @@ def tile_attend_qpk_cap_srt_kernel(tc, q_words, q_scales, k_words, k_scales, vT,
 
         def turn_scales(g, vs_row, tag, bank):
             vs_placed = held.tile([P, PACK, P], F32, name="vs_placed%d" % g, tag=tag, align_bytes=64)
-            for u in range(2):
-                nc.scalar.copy(place_pair(vs_placed, u), by_place(vs_row[:], u))
+            nc.scalar.copy(
+                vs_placed[:].rearrange("r (u h) (b j) -> r u h b j", u=2, j=8),
+                vs_row[:].rearrange("r (b u j h) -> r u h b j", u=2, j=8, h=2),
+            )
             vs_turned = psum.tile([P, PACK, P], F32, name="vs_turned%d" % g, tag=bank)
             for t in range(PACK):
                 nc.tensor.transpose(vs_turned[:, t, :], vs_placed[:, t, :], ident[:])
@@ -105,15 +102,16 @@ def tile_attend_qpk_cap_srt_kernel(tc, q_words, q_scales, k_words, k_scales, vT,
             return col
 
         ks_listed = held.tile([P, N], U8, name="ks_listed", align_bytes=64)
-        nc.vector.tensor_copy(ks_listed[:], ks_pool[:].indirect(offsets[:]))
+        nc.vector.tensor_copy(ks_listed[:], ks_pool[:, 0:T].indirect(offsets[:]))
         for r in range(4):
-            nc.sync.dma_start(planes[r:P:32, 0:N].bitcast(I32), ks_listed[8 * r : P : 32, :].bitcast(I32))
-        load_columns(v_pool, vT, 512, reach(0))
+            nc.sync.dma_start(planes[r:P:32, 0:N].bitcast(I32), ks_listed[48 + r : 64 : 4, :].bitcast(I32))
+        load_columns(v_pool, vT, 0, reach(0))
         load_columns(v_pool, vT, reach(0), T)
 
-        early_row = gather_scales(0, "vs_row")
+        vs_slot = [turn_scales(0, gather_scales(0, "vs_row0"), "vs_placed0", "turn1")]
+        late_row = gather_scales(1, "vs_row1")
 
-        tanh_all = held.tile([P, PASSES, PACK, P], F32, name="tanh_all", align_bytes=64)
+        tanh_all = held.tile([P, N], F32, name="tanh_all", tag="tanh_all", align_bytes=64)
         for g in range(PASSES):
             k_codes = held.tile([P, PASS], I32, name="k_listed%d" % g, tag="listed%d" % g, align_bytes=64)[:]
             nc.vector.tensor_copy(k_codes.bitcast(U32), k_pool[:, 0 : reach(g)].bitcast(U32).indirect(slots(g)))
@@ -130,19 +128,17 @@ def tile_attend_qpk_cap_srt_kernel(tc, q_words, q_scales, k_words, k_scales, vT,
                     start=True,
                     stop=True,
                 )
-                for u in range(2):
-                    rows = tanh_all[:, g, :, c * width // PACK : (c + 1) * width // PACK]
-                    nc.scalar.activation(place_pair(rows, u), by_place(score[:], u), ACT.Tanh, scale=1.0 / CAP)
+                lo = g * PASS + c * width
+                nc.scalar.activation(tanh_all[:, lo : lo + width], score[:], ACT.Tanh, scale=1.0 / CAP)
 
-        vs_slot = [turn_scales(0, early_row, "vs_placed", "score00")]
-        late_row = gather_scales(1, "k_pool")
+        vs_slot.append(turn_scales(1, late_row, "vs_placed1", "score00"))
 
         neg_c = held.tile([P, N], F32, name="neg_c", align_bytes=64)
         least = [held.tile([P, 1], F32, name="least%d" % g) for g in range(PASSES)]
         for g in range(PASSES):
             nc.vector.tensor_scalar(
                 neg_c[:, g * PASS : (g + 1) * PASS],
-                tanh_all[:, g].rearrange("q t s -> q (t s)"),
+                tanh_all[:, g * PASS : (g + 1) * PASS],
                 -CAP,
                 least[g - 1][:] if g else None,
                 ALU.mult,
@@ -151,17 +147,19 @@ def tile_attend_qpk_cap_srt_kernel(tc, q_words, q_scales, k_words, k_scales, vT,
             )
         neg_m = least[PASSES - 1][:]
 
-        vs_slot.append(turn_scales(1, late_row, "listed1", "turn1"))
-
         turned = []
         sums = held.tile([P, 2 * PASSES], F32, name="sums")
         for g in range(PASSES):
             p_turned = psum.tile([P, PACK, P], F32, name="p_turned%d" % g, tag="turn%d" % g)
             for u in range(2):
                 p = held.tile([P, 2 * P], F32, name="p%d%d" % (g, u), align_bytes=64)
-                lo = g * PASS + u * 2 * P
                 nc.scalar.activation(
-                    p[:], neg_c[:, lo : lo + 2 * P], ACT.Exp, bias=neg_m, scale=-1.0, accum_out=sums[:, 2 * g + u : 2 * g + u + 1]
+                    p[:].rearrange("q (h b j) -> q h b j", h=2, j=8),
+                    by_place(neg_c[:, g * PASS : (g + 1) * PASS], u),
+                    ACT.Exp,
+                    bias=neg_m,
+                    scale=-1.0,
+                    accum_out=sums[:, 2 * g + u : 2 * g + u + 1],
                 )
                 for h in range(2):
                     nc.tensor.transpose(p_turned[:, 2 * u + h, :], p[:, h * P : (h + 1) * P], ident[:])
@@ -171,7 +169,7 @@ def tile_attend_qpk_cap_srt_kernel(tc, q_words, q_scales, k_words, k_scales, vT,
 
         v_turned = []
         for g in range(PASSES):
-            v_pairs = held.tile([P, PASS], BF16, name="v_pairs%d" % g, tag=("k_pool", "v_pairs1")[g], align_bytes=64)[:]
+            v_pairs = held.tile([P, PASS], BF16, name="v_pairs%d" % g, tag=("tanh_all", "v_pairs1")[g], align_bytes=64)[:]
             nc.vector.tensor_copy(
                 v_pairs.rearrange("e (u b x) -> e b u x", u=2, x=16), v_pool[:, 0 : reach(g)].indirect(slots(g))
             )

@@ -64,17 +64,16 @@ def tile_attend_qpk_cap_srt_kernel(tc, q_words, q_scales, k_words, k_scales, vT,
         def load_query_scales(r):
             nc.sync.dma_start(planes[r:P:32, N : N + NQ].bitcast(I32), q_scales[0, 0, r:16:4, :].bitcast(I32))
 
-        nc.sync.dma_start(ks_pool[48:64, 0:T].bitcast(I32), k_scales[0].bitcast(I32))
         nc.sync.dma_start(offsets[:], offs)
+        nc.sync.dma_start(ks_pool[48:64, 0:T].bitcast(I32), k_scales[0].bitcast(I32))
         load_columns(k_pool, k_source, 0, 1536)
         nc.sync.dma_start(vs_pool[P - 1 : P, :], vs[0:1, :])
-        q_codes = held.tile([P, NQ], I32, name="q_codes", align_bytes=64)
-        nc.sync.dma_start(q_codes[:], q_words[0, 0].rearrange("p n t -> p (n t)").bitcast(I32))
-        for r in range(3):
+        for r in range(4):
             load_query_scales(r)
         load_columns(k_pool, k_source, 1536, reach(0))
         load_columns(k_pool, k_source, reach(0), T)
-        load_query_scales(3)
+        q_codes = held.tile([P, NQ], I32, name="q_codes", align_bytes=64)
+        nc.sync.dma_start(q_codes[:], q_words[0, 0].rearrange("p n t -> p (n t)").bitcast(I32))
         v_pool = held.tile([P, T], F32, name="v_pool", tag="v_pool", align_bytes=64)
 
         ident = held.tile([P, P], F32, name="ident", align_bytes=64)
@@ -134,18 +133,19 @@ def tile_attend_qpk_cap_srt_kernel(tc, q_words, q_scales, k_words, k_scales, vT,
         vs_slot.append(turn_scales(1, late_row, "vs_placed1", "score00"))
 
         neg_c = held.tile([P, N], F32, name="neg_c", align_bytes=64)
-        least = [held.tile([P, 1], F32, name="least%d" % g) for g in range(PASSES)]
-        for g in range(PASSES):
+        cuts = (0, PASS, N)
+        least = [held.tile([P, 1], F32, name="least%d" % i) for i in range(2)]
+        for i in range(2):
             nc.vector.tensor_scalar(
-                neg_c[:, g * PASS : (g + 1) * PASS],
-                tanh_all[:, g * PASS : (g + 1) * PASS],
+                neg_c[:, cuts[i] : cuts[i + 1]],
+                tanh_all[:, cuts[i] : cuts[i + 1]],
                 -CAP,
-                least[g - 1][:] if g else None,
+                least[i - 1][:] if i else None,
                 ALU.mult,
                 ALU.min,
-                accum_out=least[g][:],
+                accum_out=least[i][:],
             )
-        neg_m = least[PASSES - 1][:]
+        neg_m = least[-1][:]
 
         turned = []
         sums = held.tile([P, 2 * PASSES], F32, name="sums")
@@ -169,7 +169,7 @@ def tile_attend_qpk_cap_srt_kernel(tc, q_words, q_scales, k_words, k_scales, vT,
 
         v_turned = []
         for g in range(PASSES):
-            v_pairs = held.tile([P, PASS], BF16, name="v_pairs%d" % g, tag=("tanh_all", "v_pairs1")[g], align_bytes=64)[:]
+            v_pairs = held.tile([P, PASS], BF16, name="v_pairs%d" % g, tag="v_pairs%d" % g, align_bytes=64)[:]
             nc.vector.tensor_copy(
                 v_pairs.rearrange("e (u b x) -> e b u x", u=2, x=16), v_pool[:, 0 : reach(g)].indirect(slots(g))
             )
@@ -178,8 +178,12 @@ def tile_attend_qpk_cap_srt_kernel(tc, q_words, q_scales, k_words, k_scales, vT,
                 nc.tensor.transpose(bank[:, u, :], v_pairs.bitcast(F32)[:, u * P : (u + 1) * P], ident[:])
             v_turned.append(bank)
 
-        late = held.tile([P, N + 2], BF16, name="late", tag="v_pool", align_bytes=64)
-        inv_sum = late[:, N : N + 2].bitcast(F32)
+        late = held.tile([P, N], BF16, name="late", tag="v_pool", align_bytes=64)
+        inv_tile = held.tile([P, 1], F32, name="inv_sum")
+        inv_sum = inv_tile[:]
+        minus_one = held.tile([P, 1], F32, name="minus_one")
+        nc.gpsimd.memset(minus_one[:], -1.0)
+        nc.gpsimd.tensor_tensor(inv_sum, row_sum[:], minus_one[:], ALU.pow)
         v_grouped = []
         for g in range(PASSES):
             grouped = held.tile([P, PASS], BF16, name="v_grouped%d" % g, align_bytes=64)
@@ -193,7 +197,6 @@ def tile_attend_qpk_cap_srt_kernel(tc, q_words, q_scales, k_words, k_scales, vT,
                 vs_slot[g][:].unsqueeze(1).to_broadcast([P, NQ, PACK]),
                 ALU.mult,
             )
-        nc.vector.reciprocal(inv_sum, row_sum[:])
 
         w_codes = held.tile([P, PASSES, NQ], U32, name="w_codes", align_bytes=64)
         v_codes = held.tile([P, PASSES, DV], U32, name="v_codes", tag="vs_slot0", align_bytes=64)
@@ -203,7 +206,6 @@ def tile_attend_qpk_cap_srt_kernel(tc, q_words, q_scales, k_words, k_scales, vT,
             nc.vector.quantize_mx(
                 out=w_codes[:, g, :].bitcast(FP8X4), scales=w_plane[:, g, :], in_=late[:, g * PASS : (g + 1) * PASS]
             )
-        for g in range(PASSES):
             nc.vector.quantize_mx(out=v_codes[:, g, :].bitcast(FP8X4), scales=v_plane[:, g, :], in_=v_grouped[g][:])
 
         acc = psum.tile([P, DV], F32, name="acc")

@@ -87,28 +87,27 @@ def tile_attend_qpk_cap_srt_kernel(tc, q_words, q_scales, k_words, k_scales, vT,
             nc.vector.tensor_copy(vs_row[:], vs_pool[:, 0 : reach(g)].indirect(slots(g)))
             return vs_row
 
-        def turn_scales(g, vs_row, tag, bank):
-            vs_placed = held.tile([P, PACK, P], F32, name="vs_placed%d" % g, tag=tag, align_bytes=64)
+        def place_scales(g, vs_row):
+            vs_placed = held.tile([P, PASS], F32, name="vs_placed%d" % g, align_bytes=64)
             nc.scalar.copy(
-                vs_placed[:].rearrange("r (u h) (b j) -> r u h b j", u=2, j=8),
-                vs_row[:].rearrange("r (b u j h) -> r u h b j", u=2, j=8, h=2),
+                vs_placed[96:P, :].rearrange("r (b j u h) -> r b j u h", u=2, j=8, h=2),
+                vs_row[96:P, :].rearrange("r (b u j h) -> r b j u h", u=2, j=8, h=2),
             )
-            vs_turned = psum.tile([P, PACK, P], F32, name="vs_turned%d" % g, tag=bank)
-            for t in range(PACK):
-                nc.tensor.transpose(vs_turned[:, t, :], vs_placed[:, t, :], ident[:])
+            return vs_placed
+
+        def deal_scales(g, vs_placed):
             col = held.tile([P, PACK], F32, name="vs_slot%d" % g, tag="vs_slot%d" % g, align_bytes=64)
-            nc.scalar.copy(col[:], vs_turned[:, :, P - 1])
+            nc.sync.dma_start(col[:], vs_placed[P - 1 : P, :])
             return col
 
         ks_listed = held.tile([P, N], U8, name="ks_listed", align_bytes=64)
         nc.vector.tensor_copy(ks_listed[:], ks_pool[:, 0:T].indirect(offsets[:]))
         for r in range(4):
             nc.sync.dma_start(planes[r:P:32, 0:N].bitcast(I32), ks_listed[48 + r : 64 : 4, :].bitcast(I32))
+
         load_columns(v_pool, vT, 0, reach(0))
         load_columns(v_pool, vT, reach(0), T)
-
-        vs_slot = [turn_scales(0, gather_scales(0, "vs_row0"), "vs_placed0", "turn1")]
-        late_row = gather_scales(1, "vs_row1")
+        vs_slot = [deal_scales(g, place_scales(g, gather_scales(g, "vs_row%d" % g))) for g in range(PASSES)]
 
         tanh_all = held.tile([P, N], F32, name="tanh_all", tag="tanh_all", align_bytes=64)
         for g in range(PASSES):
@@ -130,7 +129,6 @@ def tile_attend_qpk_cap_srt_kernel(tc, q_words, q_scales, k_words, k_scales, vT,
                 lo = g * PASS + c * width
                 nc.scalar.activation(tanh_all[:, lo : lo + width], score[:], ACT.Tanh, scale=1.0 / CAP)
 
-        vs_slot.append(turn_scales(1, late_row, "vs_placed1", "score00"))
 
         neg_c = held.tile([P, N], F32, name="neg_c", align_bytes=64)
         cuts = (0, PASS, N)
@@ -178,7 +176,7 @@ def tile_attend_qpk_cap_srt_kernel(tc, q_words, q_scales, k_words, k_scales, vT,
                 nc.tensor.transpose(bank[:, u, :], v_pairs.bitcast(F32)[:, u * P : (u + 1) * P], ident[:])
             v_turned.append(bank)
 
-        late = held.tile([P, N], BF16, name="late", tag="v_pool", align_bytes=64)
+        late = held.tile([P, N], BF16, name="late", align_bytes=64)
         inv_tile = held.tile([P, 1], F32, name="inv_sum")
         inv_sum = inv_tile[:]
         minus_one = held.tile([P, 1], F32, name="minus_one")

@@ -13,7 +13,18 @@ CAP = 2.0
 PACK = 4
 PASS = P * PACK
 PASSES = N // PASS
+HALF = PASS // 2
 LIST_COLS = PASS // 16
+SCALE_ROWS = 16
+QUADRANT = 32
+
+KS_END = 64
+KS_FIRST = KS_END - SCALE_ROWS
+VS_ROW = P - 1
+LAST_QUADRANT = P - QUADRANT
+VS_FILL_VECTOR = 704
+KEYS_FIRST = 1536
+SPARE = 4
 
 FLOPS = 2 * NQ * N * (D + DV)
 
@@ -42,146 +53,133 @@ def tile_attend_qpk_cap_srt_kernel(tc, q_words, q_scales, k_words, k_scales, vT,
         def slots(g):
             return offsets[:, g * LIST_COLS : (g + 1) * LIST_COLS]
 
-        ks_pool = held.tile([P, T + 4], U8, name="ks_pool", align_bytes=64)
-        planes = held.tile([P, N + NQ + 4], U8, name="planes", align_bytes=64)
+        def pass_cols(g):
+            return slice(g * PASS, (g + 1) * PASS)
+
+        ks_pool = held.tile([P, T + SPARE], U8, name="ks_pool", align_bytes=64)
+        planes = held.tile([P, N + NQ + SPARE], U8, name="planes", align_bytes=64)
         vs_pool = held.tile([P, T], F32, name="vs_pool", align_bytes=64)
         nc.vector.memset(planes[:].bitcast(I32), 0)
-        nc.vector.memset(ks_pool[0:48, :].bitcast(I32), 0)
-        nc.gpsimd.memset(ks_pool[64:P, 0:T].bitcast(I32), 0)
-        nc.vector.memset(vs_pool[0 : P - 1, 0:1], 0.0)
-        nc.vector.memset(vs_pool[0 : P - 1, 1:704], 0.0)
-        nc.gpsimd.memset(vs_pool[0 : P - 1, 704 : reach(0)], 0.0)
-        nc.gpsimd.memset(vs_pool[0 : P - 1, reach(0) : T], 0.0)
+        nc.vector.memset(ks_pool[0:KS_FIRST, :].bitcast(I32), 0)
+        nc.gpsimd.memset(ks_pool[KS_END:P, 0:T].bitcast(I32), 0)
+        nc.vector.memset(vs_pool[0:VS_ROW, 0:1], 0.0)
+        nc.vector.memset(vs_pool[0:VS_ROW, 1:VS_FILL_VECTOR], 0.0)
+        nc.gpsimd.memset(vs_pool[0:VS_ROW, VS_FILL_VECTOR : reach(0)], 0.0)
+        nc.gpsimd.memset(vs_pool[0:VS_ROW, reach(0) : T], 0.0)
         k_plane = planes[:, 0:N]
         q_plane = planes[:, N : N + NQ]
 
         def load_columns(pool_tile, source, lo, hi):
             nc.sync.dma_start(pool_tile[:, lo:hi], source[:, lo:hi])
 
-        k_pool = held.tile([P, T], I32, name="k_pool", tag="k_pool", align_bytes=64)
+        k_pool = held.tile([P, T], I32, name="k_pool", align_bytes=64)
         k_source = k_words[0].rearrange("p n t -> p (n t)").bitcast(I32)
-
-        def load_query_scales(r):
-            nc.sync.dma_start(planes[r:P:32, N : N + NQ].bitcast(I32), q_scales[0, 0, r:16:4, :].bitcast(I32))
-
         nc.sync.dma_start(offsets[:], offs)
-        nc.sync.dma_start(ks_pool[48:64, 0:T].bitcast(I32), k_scales[0].bitcast(I32))
-        load_columns(k_pool, k_source, 0, 1536)
-        nc.sync.dma_start(vs_pool[P - 1 : P, :], vs[0:1, :])
-        for r in range(4):
-            load_query_scales(r)
-        load_columns(k_pool, k_source, 1536, reach(0))
+        nc.sync.dma_start(ks_pool[KS_FIRST:KS_END, 0:T].bitcast(I32), k_scales[0].bitcast(I32))
+        load_columns(k_pool, k_source, 0, KEYS_FIRST)
+        nc.sync.dma_start(vs_pool[VS_ROW:P, :], vs[0:1, :])
+        for r in range(PACK):
+            nc.sync.dma_start(
+                planes[r:P:QUADRANT, N : N + NQ].bitcast(I32), q_scales[0, 0, r:SCALE_ROWS:PACK, :].bitcast(I32)
+            )
+        load_columns(k_pool, k_source, KEYS_FIRST, reach(0))
         load_columns(k_pool, k_source, reach(0), T)
         q_codes = held.tile([P, NQ], I32, name="q_codes", align_bytes=64)
-        nc.sync.dma_start(q_codes[:], q_words[0, 0].rearrange("p n t -> p (n t)").bitcast(I32))
-        v_pool = held.tile([P, T], F32, name="v_pool", tag="v_pool", align_bytes=64)
+        v_pool = held.tile([P, T], F32, name="v_pool", align_bytes=64)
 
         ident = held.tile([P, P], F32, name="ident", align_bytes=64)
         make_identity(nc, ident[:])
 
-        def by_place(listed, u):
-            return listed.rearrange("r (b u j h) -> r u h b j", u=2, j=8, h=2)[:, u]
-
-        def gather_scales(g, tag):
-            vs_row = held.tile([P, PASS], F32, name="vs_row%d" % g, tag=tag, align_bytes=64)
-            nc.vector.tensor_copy(vs_row[:], vs_pool[:, 0 : reach(g)].indirect(slots(g)))
-            return vs_row
-
-        def place_scales(g, vs_row):
-            vs_placed = held.tile([P, PASS], F32, name="vs_placed%d" % g, align_bytes=64)
-            nc.scalar.copy(
-                vs_placed[96:P, :].rearrange("r (b j u h) -> r b j u h", u=2, j=8, h=2),
-                vs_row[96:P, :].rearrange("r (b u j h) -> r b j u h", u=2, j=8, h=2),
-            )
-            return vs_placed
-
-        def deal_scales(g, vs_placed):
-            col = held.tile([P, PACK], F32, name="vs_slot%d" % g, tag="vs_slot%d" % g, align_bytes=64)
-            nc.sync.dma_start(col[:], vs_placed[P - 1 : P, :])
-            return col
-
         ks_listed = held.tile([P, N], U8, name="ks_listed", align_bytes=64)
         nc.vector.tensor_copy(ks_listed[:], ks_pool[:, 0:T].indirect(offsets[:]))
-        for r in range(4):
-            nc.sync.dma_start(planes[r:P:32, 0:N].bitcast(I32), ks_listed[48 + r : 64 : 4, :].bitcast(I32))
-
+        for r in range(PACK):
+            nc.sync.dma_start(
+                planes[r:P:QUADRANT, 0:N].bitcast(I32), ks_listed[KS_FIRST + r : KS_END : PACK, :].bitcast(I32)
+            )
+        nc.sync.dma_start(q_codes[:], q_words[0, 0].rearrange("p n t -> p (n t)").bitcast(I32))
         load_columns(v_pool, vT, 0, reach(0))
         load_columns(v_pool, vT, reach(0), T)
-        vs_slot = [deal_scales(g, place_scales(g, gather_scales(g, "vs_row%d" % g))) for g in range(PASSES)]
 
-        tanh_all = held.tile([P, N], F32, name="tanh_all", tag="tanh_all", align_bytes=64)
+        vs_slot = []
         for g in range(PASSES):
-            k_codes = held.tile([P, PASS], I32, name="k_listed%d" % g, tag="listed%d" % g, align_bytes=64)[:]
+            vs_listed = held.tile([P, PASS], F32, name="vs_listed%d" % g, align_bytes=64)
+            nc.vector.tensor_copy(vs_listed[:], vs_pool[:, 0 : reach(g)].indirect(slots(g)))
+            vs_placed = held.tile([P, PASS], F32, name="vs_placed%d" % g, align_bytes=64)
+            nc.scalar.copy(
+                vs_placed[LAST_QUADRANT:P, :].rearrange("r (b j u h) -> r b j u h", u=2, j=8, h=2),
+                vs_listed[LAST_QUADRANT:P, :].rearrange("r (b u j h) -> r b j u h", u=2, j=8, h=2),
+            )
+            dealt = held.tile([P, PACK], F32, name="vs_slot%d" % g, tag="vs_slot%d" % g, align_bytes=64)
+            nc.sync.dma_start(dealt[:], vs_placed[VS_ROW:P, :])
+            vs_slot.append(dealt)
+
+        tanh_all = held.tile([P, N], F32, name="tanh_all", align_bytes=64)
+        for g in range(PASSES):
+            k_codes = held.tile([P, PASS], I32, name="k_listed%d" % g, align_bytes=64)[:]
             nc.vector.tensor_copy(k_codes.bitcast(U32), k_pool[:, 0 : reach(g)].bitcast(U32).indirect(slots(g)))
-            pieces = g + 1
-            width = PASS // pieces
-            for c in range(pieces):
-                score = psum.tile([P, width], F32, name="score%d%d" % (g, c), tag="score%d%d" % (g, c))
+            for c in range(2):
+                lo = g * PASS + c * HALF
+                score = psum.tile([P, HALF], F32, name="score%d%d" % (g, c), tag="score%d%d" % (g, c))
                 nc.tensor.matmul_mx(
                     out=score[:],
                     lhsT=q_codes[:].bitcast(FP8X4),
                     lhsT_scale=q_plane,
-                    rhs=k_codes[:, c * width : (c + 1) * width].bitcast(FP8X4),
-                    rhs_scale=k_plane[:, g * PASS + c * width : g * PASS + (c + 1) * width],
+                    rhs=k_codes[:, c * HALF : (c + 1) * HALF].bitcast(FP8X4),
+                    rhs_scale=k_plane[:, lo : lo + HALF],
                     start=True,
                     stop=True,
                 )
-                lo = g * PASS + c * width
-                nc.scalar.activation(tanh_all[:, lo : lo + width], score[:], ACT.Tanh, scale=1.0 / CAP)
-
+                nc.scalar.activation(tanh_all[:, lo : lo + HALF], score[:], ACT.Tanh, scale=1.0 / CAP)
 
         neg_c = held.tile([P, N], F32, name="neg_c", align_bytes=64)
-        cuts = (0, PASS, N)
-        least = [held.tile([P, 1], F32, name="least%d" % i) for i in range(2)]
-        for i in range(2):
+        least = [held.tile([P, 1], F32, name="least%d" % g) for g in range(PASSES)]
+        for g in range(PASSES):
             nc.vector.tensor_scalar(
-                neg_c[:, cuts[i] : cuts[i + 1]],
-                tanh_all[:, cuts[i] : cuts[i + 1]],
+                neg_c[:, pass_cols(g)],
+                tanh_all[:, pass_cols(g)],
                 -CAP,
-                least[i - 1][:] if i else None,
+                least[g - 1][:] if g else None,
                 ALU.mult,
                 ALU.min,
-                accum_out=least[i][:],
+                accum_out=least[g][:],
             )
-        neg_m = least[-1][:]
+        neg_m = least[PASSES - 1][:]
 
-        turned = []
+        p_turned = []
         sums = held.tile([P, 2 * PASSES], F32, name="sums")
         for g in range(PASSES):
-            p_turned = psum.tile([P, PACK, P], F32, name="p_turned%d" % g, tag="turn%d" % g)
+            bank = psum.tile([P, PACK, NQ], F32, name="p_turned%d" % g)
+            by_place = neg_c[:, pass_cols(g)].rearrange("q (b u j h) -> q u h b j", u=2, j=8, h=2)
             for u in range(2):
-                p = held.tile([P, 2 * P], F32, name="p%d%d" % (g, u), align_bytes=64)
+                p = held.tile([P, HALF], F32, name="p%d%d" % (g, u), align_bytes=64)
                 nc.scalar.activation(
                     p[:].rearrange("q (h b j) -> q h b j", h=2, j=8),
-                    by_place(neg_c[:, g * PASS : (g + 1) * PASS], u),
+                    by_place[:, u],
                     ACT.Exp,
                     bias=neg_m,
                     scale=-1.0,
                     accum_out=sums[:, 2 * g + u : 2 * g + u + 1],
                 )
                 for h in range(2):
-                    nc.tensor.transpose(p_turned[:, 2 * u + h, :], p[:, h * P : (h + 1) * P], ident[:])
-            turned.append(p_turned)
+                    nc.tensor.transpose(bank[:, 2 * u + h, :], p[:, h * P : (h + 1) * P], ident[:])
+            p_turned.append(bank)
         row_sum = held.tile([P, 1], F32, name="row_sum")
         nc.scalar.activation(sums[:], sums[:], ACT.Identity, accum_out=row_sum[:])
 
         v_turned = []
         for g in range(PASSES):
-            v_pairs = held.tile([P, PASS], BF16, name="v_pairs%d" % g, tag="v_pairs%d" % g, align_bytes=64)[:]
+            v_pairs = held.tile([P, PASS], BF16, name="v_pairs%d" % g, align_bytes=64)[:]
             nc.vector.tensor_copy(
                 v_pairs.rearrange("e (u b x) -> e b u x", u=2, x=16), v_pool[:, 0 : reach(g)].indirect(slots(g))
             )
-            bank = psum.tile([P, 2, P], F32, name="v_turned%d" % g)
+            bank = psum.tile([P, 2, DV], F32, name="v_turned%d" % g)
             for u in range(2):
                 nc.tensor.transpose(bank[:, u, :], v_pairs.bitcast(F32)[:, u * P : (u + 1) * P], ident[:])
             v_turned.append(bank)
 
-        late = held.tile([P, N], BF16, name="late", align_bytes=64)
-        inv_tile = held.tile([P, 1], F32, name="inv_sum")
-        inv_sum = inv_tile[:]
-        minus_one = held.tile([P, 1], F32, name="minus_one")
-        nc.gpsimd.memset(minus_one[:], -1.0)
-        nc.gpsimd.tensor_tensor(inv_sum, row_sum[:], minus_one[:], ALU.pow)
+        weights = held.tile([P, N], BF16, name="weights", align_bytes=64)
+        inv_sum = held.tile([P, 1], F32, name="inv_sum", tag="vs_slot1", align_bytes=64)
+        nc.vector.reciprocal(inv_sum[:], row_sum[:])
         v_grouped = []
         for g in range(PASSES):
             grouped = held.tile([P, PASS], BF16, name="v_grouped%d" % g, align_bytes=64)
@@ -190,8 +188,8 @@ def tile_attend_qpk_cap_srt_kernel(tc, q_words, q_scales, k_words, k_scales, vT,
             )
             v_grouped.append(grouped)
             nc.vector.tensor_tensor(
-                late[:, g * PASS : (g + 1) * PASS].rearrange("s (q t) -> s q t", t=PACK),
-                turned[g][:].rearrange("s t q -> s q t"),
+                weights[:, pass_cols(g)].rearrange("s (q t) -> s q t", t=PACK),
+                p_turned[g][:].rearrange("s t q -> s q t"),
                 vs_slot[g][:].unsqueeze(1).to_broadcast([P, NQ, PACK]),
                 ALU.mult,
             )
@@ -201,12 +199,10 @@ def tile_attend_qpk_cap_srt_kernel(tc, q_words, q_scales, k_words, k_scales, vT,
         w_plane = held.tile([P, PASSES, NQ], U8, name="w_plane", align_bytes=64)
         v_plane = held.tile([P, PASSES, DV], U8, name="v_plane", align_bytes=64)
         for g in range(PASSES):
-            nc.vector.quantize_mx(
-                out=w_codes[:, g, :].bitcast(FP8X4), scales=w_plane[:, g, :], in_=late[:, g * PASS : (g + 1) * PASS]
-            )
+            nc.vector.quantize_mx(out=w_codes[:, g, :].bitcast(FP8X4), scales=w_plane[:, g, :], in_=weights[:, pass_cols(g)])
             nc.vector.quantize_mx(out=v_codes[:, g, :].bitcast(FP8X4), scales=v_plane[:, g, :], in_=v_grouped[g][:])
 
-        acc = psum.tile([P, DV], F32, name="acc")
+        acc = psum.tile([P, DV], F32, name="acc", tag="score00")
         for g in range(PASSES):
             nc.tensor.matmul_mx(
                 out=acc[:],
@@ -219,5 +215,5 @@ def tile_attend_qpk_cap_srt_kernel(tc, q_words, q_scales, k_words, k_scales, vT,
             )
 
         result = held.tile([P, DV], F32, name="result", align_bytes=64)
-        nc.scalar.activation(result[:], acc[:], ACT.Copy, scale=inv_sum)
+        nc.scalar.activation(result[:], acc[:], ACT.Copy, scale=inv_sum[:])
         nc.sync.dma_start(out[0], result[:])

@@ -56,6 +56,10 @@ def tile_attend_qpk_cap_srt_kernel(tc, q_words, q_scales, k_words, k_scales, vT,
         def pass_cols(g):
             return slice(g * PASS, (g + 1) * PASS)
 
+        warm = held.tile([P, 2], F32, name="warm")
+        nc.gpsimd.memset(warm[:, 0:1], 0.0)
+        nc.scalar.activation(warm[:, 1:2], warm[:, 0:1], ACT.Tanh)
+
         ks_pool = held.tile([P, T + SPARE], U8, name="ks_pool", align_bytes=64)
         planes = held.tile([P, N + NQ + SPARE], U8, name="planes", align_bytes=64)
         vs_pool = held.tile([P, T], F32, name="vs_pool", align_bytes=64)
@@ -76,8 +80,8 @@ def tile_attend_qpk_cap_srt_kernel(tc, q_words, q_scales, k_words, k_scales, vT,
         k_source = k_words[0].rearrange("p n t -> p (n t)").bitcast(I32)
         nc.sync.dma_start(offsets[:], offs)
         nc.sync.dma_start(ks_pool[KS_FIRST:KS_END, 0:T].bitcast(I32), k_scales[0].bitcast(I32))
-        load_columns(k_pool, k_source, 0, KEYS_FIRST)
         nc.sync.dma_start(vs_pool[VS_ROW:P, :], vs[0:1, :])
+        load_columns(k_pool, k_source, 0, KEYS_FIRST)
         for r in range(PACK):
             nc.sync.dma_start(
                 planes[r:P:QUADRANT, N : N + NQ].bitcast(I32), q_scales[0, 0, r:SCALE_ROWS:PACK, :].bitcast(I32)
@@ -100,36 +104,36 @@ def tile_attend_qpk_cap_srt_kernel(tc, q_words, q_scales, k_words, k_scales, vT,
         load_columns(v_pool, vT, 0, reach(0))
         load_columns(v_pool, vT, reach(0), T)
 
-        vs_slot = []
-        for g in range(PASSES):
-            vs_listed = held.tile([P, PASS], F32, name="vs_listed%d" % g, align_bytes=64)
-            nc.vector.tensor_copy(vs_listed[:], vs_pool[:, 0 : reach(g)].indirect(slots(g)))
-            vs_placed = held.tile([P, PASS], F32, name="vs_placed%d" % g, align_bytes=64)
-            nc.scalar.copy(
-                vs_placed[LAST_QUADRANT:P, :].rearrange("r (b j u h) -> r b j u h", u=2, j=8, h=2),
-                vs_listed[LAST_QUADRANT:P, :].rearrange("r (b u j h) -> r b j u h", u=2, j=8, h=2),
+        vs_listed = [held.tile([P, PASS], F32, name="vs_listed%d" % g, align_bytes=64) for g in range(PASSES)]
+        nc.vector.tensor_copy(vs_listed[0][:], vs_pool[:, 0 : reach(0)].indirect(slots(0)))
+        nc.scalar.activation(vs_listed[1][:], vs_pool[:].indirect(slots(1)), ACT.Copy)
+        vs_row = held.tile([P, P, PASSES, PACK], F32, name="vs_row", tag="vs_row", align_bytes=64)
+        for g, place in enumerate((nc.vector.tensor_copy, nc.scalar.copy)):
+            place(
+                vs_row[LAST_QUADRANT:P, :, g, :].rearrange("r (b j) (u h) -> r b j u h", j=8, u=2),
+                vs_listed[g][LAST_QUADRANT:P, :].rearrange("r (b u j h) -> r b j u h", u=2, j=8, h=2),
             )
-            dealt = held.tile([P, PACK], F32, name="vs_slot%d" % g, tag="vs_slot%d" % g, align_bytes=64)
-            nc.sync.dma_start(dealt[:], vs_placed[VS_ROW:P, :])
-            vs_slot.append(dealt)
+        vs_slot = held.tile([P, PASSES, PACK], F32, name="vs_slot", tag="vs_slot", align_bytes=64)
+        nc.sync.dma_start(vs_slot[:].rearrange("s g t -> s (g t)"), vs_row[VS_ROW:P].rearrange("r s g t -> r (s g t)"))
 
         tanh_all = held.tile([P, N], F32, name="tanh_all", align_bytes=64)
-        for g in range(PASSES):
-            k_codes = held.tile([P, PASS], I32, name="k_listed%d" % g, align_bytes=64)[:]
-            nc.vector.tensor_copy(k_codes.bitcast(U32), k_pool[:, 0 : reach(g)].bitcast(U32).indirect(slots(g)))
-            for c in range(2):
-                lo = g * PASS + c * HALF
-                score = psum.tile([P, HALF], F32, name="score%d%d" % (g, c), tag="score%d%d" % (g, c))
+        k_window = k_pool[:].bitcast(U32)
+        for lo, hi, tokens in ((0, PASS, reach(0)), (PASS, PASS + HALF, T), (PASS + HALF, N, T)):
+            k_listed = held.tile([P, hi - lo], I32, name="k_listed%d" % lo, align_bytes=64)
+            listed = offsets[:, lo * LIST_COLS // PASS : hi * LIST_COLS // PASS]
+            nc.vector.tensor_copy(k_listed[:].bitcast(U32), k_window[:, 0:tokens].indirect(listed))
+            for c in range(lo, hi, HALF):
+                score = psum.tile([P, HALF], F32, name="score%d" % c, tag="score%d" % c)
                 nc.tensor.matmul_mx(
                     out=score[:],
                     lhsT=q_codes[:].bitcast(FP8X4),
                     lhsT_scale=q_plane,
-                    rhs=k_codes[:, c * HALF : (c + 1) * HALF].bitcast(FP8X4),
-                    rhs_scale=k_plane[:, lo : lo + HALF],
+                    rhs=k_listed[:, c - lo : c - lo + HALF].bitcast(FP8X4),
+                    rhs_scale=k_plane[:, c : c + HALF],
                     start=True,
                     stop=True,
                 )
-                nc.scalar.activation(tanh_all[:, lo : lo + HALF], score[:], ACT.Tanh, scale=1.0 / CAP)
+                nc.scalar.activation(tanh_all[:, c : c + HALF], score[:], ACT.Tanh, scale=1.0 / CAP)
 
         neg_c = held.tile([P, N], F32, name="neg_c", align_bytes=64)
         least = [held.tile([P, 1], F32, name="least%d" % g) for g in range(PASSES)]
@@ -178,7 +182,7 @@ def tile_attend_qpk_cap_srt_kernel(tc, q_words, q_scales, k_words, k_scales, vT,
             v_turned.append(bank)
 
         weights = held.tile([P, N], BF16, name="weights", align_bytes=64)
-        inv_sum = held.tile([P, 1], F32, name="inv_sum", tag="vs_slot1", align_bytes=64)
+        inv_sum = held.tile([P, 1], F32, name="inv_sum", tag="vs_row", align_bytes=64)
         nc.vector.reciprocal(inv_sum[:], row_sum[:])
         v_grouped = []
         for g in range(PASSES):
@@ -190,19 +194,19 @@ def tile_attend_qpk_cap_srt_kernel(tc, q_words, q_scales, k_words, k_scales, vT,
             nc.vector.tensor_tensor(
                 weights[:, pass_cols(g)].rearrange("s (q t) -> s q t", t=PACK),
                 p_turned[g][:].rearrange("s t q -> s q t"),
-                vs_slot[g][:].unsqueeze(1).to_broadcast([P, NQ, PACK]),
+                vs_slot[:, g, :].unsqueeze(1).to_broadcast([P, NQ, PACK]),
                 ALU.mult,
             )
 
         w_codes = held.tile([P, PASSES, NQ], U32, name="w_codes", align_bytes=64)
-        v_codes = held.tile([P, PASSES, DV], U32, name="v_codes", tag="vs_slot0", align_bytes=64)
+        v_codes = held.tile([P, PASSES, DV], U32, name="v_codes", align_bytes=64)
         w_plane = held.tile([P, PASSES, NQ], U8, name="w_plane", align_bytes=64)
         v_plane = held.tile([P, PASSES, DV], U8, name="v_plane", align_bytes=64)
         for g in range(PASSES):
             nc.vector.quantize_mx(out=w_codes[:, g, :].bitcast(FP8X4), scales=w_plane[:, g, :], in_=weights[:, pass_cols(g)])
             nc.vector.quantize_mx(out=v_codes[:, g, :].bitcast(FP8X4), scales=v_plane[:, g, :], in_=v_grouped[g][:])
 
-        acc = psum.tile([P, DV], F32, name="acc", tag="score00")
+        acc = psum.tile([P, DV], F32, name="acc", tag="score0")
         for g in range(PASSES):
             nc.tensor.matmul_mx(
                 out=acc[:],

@@ -56,10 +56,6 @@ def tile_attend_qpk_cap_srt_kernel(tc, q_words, q_scales, k_words, k_scales, vT,
         def pass_cols(g):
             return slice(g * PASS, (g + 1) * PASS)
 
-        warm = held.tile([P, 2], F32, name="warm")
-        nc.gpsimd.memset(warm[:, 0:1], 0.0)
-        nc.scalar.activation(warm[:, 1:2], warm[:, 0:1], ACT.Tanh)
-
         ks_pool = held.tile([P, T + SPARE], U8, name="ks_pool", align_bytes=64)
         planes = held.tile([P, N + NQ + SPARE], U8, name="planes", align_bytes=64)
         vs_pool = held.tile([P, T], F32, name="vs_pool", align_bytes=64)

@@ -181,11 +181,14 @@ def tile_attend_qpk_cap_srt_kernel(tc, q_words, q_scales, k_words, k_scales, vT,
         inv_sum = held.tile([P, 1], F32, name="inv_sum", tag="vs_row", align_bytes=64)
         nc.vector.reciprocal(inv_sum[:], row_sum[:])
         v_grouped = []
+        pieces = (((0, DV),), ((0, DV // 2), (DV // 2, DV)))
         for g in range(PASSES):
             grouped = held.tile([P, PASS], BF16, name="v_grouped%d" % g, align_bytes=64)
-            nc.scalar.copy(
-                grouped[:].bitcast(F32).rearrange("s (e u) -> s e u", u=2), v_turned[g][:].rearrange("s u e -> s e u")
-            )
+            for lo, hi in pieces[g]:
+                nc.scalar.copy(
+                    grouped[:].bitcast(F32).rearrange("s (e u) -> s e u", u=2)[:, lo:hi],
+                    v_turned[g][:].rearrange("s u e -> s e u")[:, lo:hi],
+                )
             v_grouped.append(grouped)
             nc.vector.tensor_tensor(
                 weights[:, pass_cols(g)].rearrange("s (q t) -> s q t", t=PACK),
@@ -200,7 +203,12 @@ def tile_attend_qpk_cap_srt_kernel(tc, q_words, q_scales, k_words, k_scales, vT,
         v_plane = held.tile([P, PASSES, DV], U8, name="v_plane", align_bytes=64)
         for g in range(PASSES):
             nc.vector.quantize_mx(out=w_codes[:, g, :].bitcast(FP8X4), scales=w_plane[:, g, :], in_=weights[:, pass_cols(g)])
-            nc.vector.quantize_mx(out=v_codes[:, g, :].bitcast(FP8X4), scales=v_plane[:, g, :], in_=v_grouped[g][:])
+            for lo, hi in pieces[g]:
+                nc.vector.quantize_mx(
+                    out=v_codes[:, g, lo:hi].bitcast(FP8X4),
+                    scales=v_plane[:, g, lo:hi],
+                    in_=v_grouped[g][:, PACK * lo : PACK * hi],
+                )
 
         acc = psum.tile([P, DV], F32, name="acc", tag="score0")
         for g in range(PASSES):

@@ -1,7 +1,6 @@
 from contextlib import ExitStack
 
 import concourse.mybir as mybir
-from concourse.masks import make_identity
 
 P = 128
 T = 4096
@@ -22,7 +21,7 @@ KS_END = 64
 KS_FIRST = KS_END - SCALE_ROWS
 VS_ROW = P - 1
 LAST_QUADRANT = P - QUADRANT
-VS_FILL_VECTOR = 704
+VS_FILL_VECTOR = 608
 KEYS_FIRST = 1536
 SPARE = 4
 
@@ -56,47 +55,60 @@ def tile_attend_qpk_cap_srt_kernel(tc, q_words, q_scales, k_words, k_scales, vT,
         def pass_cols(g):
             return slice(g * PASS, (g + 1) * PASS)
 
+        ident = held.tile([P, P], F32, name="ident", align_bytes=64)
+        zero = held.tile([P, 1], F32, name="zero")
+        nc.gpsimd.memset(zero[:], 0.0)
+        nc.scalar.activation(ident[:], zero[:].to_broadcast([P, P]), ACT.Copy)
+
         ks_pool = held.tile([P, T + SPARE], U8, name="ks_pool", align_bytes=64)
-        planes = held.tile([P, N + NQ + SPARE], U8, name="planes", align_bytes=64)
+        k_plane = held.tile([P, N + SPARE], U8, name="k_plane", align_bytes=64)
+        q_plane = held.tile([P, NQ + SPARE], U8, name="q_plane", align_bytes=64)
         vs_pool = held.tile([P, T], F32, name="vs_pool", align_bytes=64)
-        nc.vector.memset(planes[:].bitcast(I32), 0)
+        nc.vector.memset(q_plane[:].bitcast(I32), 0)
+        nc.vector.memset(k_plane[:].bitcast(I32), 0)
         nc.vector.memset(ks_pool[0:KS_FIRST, :].bitcast(I32), 0)
         nc.gpsimd.memset(ks_pool[KS_END:P, 0:T].bitcast(I32), 0)
         nc.vector.memset(vs_pool[0:VS_ROW, 0:1], 0.0)
         nc.vector.memset(vs_pool[0:VS_ROW, 1:VS_FILL_VECTOR], 0.0)
         nc.gpsimd.memset(vs_pool[0:VS_ROW, VS_FILL_VECTOR : reach(0)], 0.0)
         nc.gpsimd.memset(vs_pool[0:VS_ROW, reach(0) : T], 0.0)
-        k_plane = planes[:, 0:N]
-        q_plane = planes[:, N : N + NQ]
 
         def load_columns(pool_tile, source, lo, hi):
             nc.sync.dma_start(pool_tile[:, lo:hi], source[:, lo:hi])
 
         k_pool = held.tile([P, T], I32, name="k_pool", align_bytes=64)
         k_source = k_words[0].rearrange("p n t -> p (n t)").bitcast(I32)
-        nc.sync.dma_start(offsets[:], offs)
         nc.sync.dma_start(ks_pool[KS_FIRST:KS_END, 0:T].bitcast(I32), k_scales[0].bitcast(I32))
-        nc.sync.dma_start(vs_pool[VS_ROW:P, :], vs[0:1, :])
+        nc.sync.dma_start(offsets[:], offs)
         load_columns(k_pool, k_source, 0, KEYS_FIRST)
+        nc.sync.dma_start(vs_pool[VS_ROW:P, :], vs[0:1, :])
         for r in range(PACK):
             nc.sync.dma_start(
-                planes[r:P:QUADRANT, N : N + NQ].bitcast(I32), q_scales[0, 0, r:SCALE_ROWS:PACK, :].bitcast(I32)
+                q_plane[r:P:QUADRANT, 0:NQ].bitcast(I32), q_scales[0, 0, r:SCALE_ROWS:PACK, :].bitcast(I32)
             )
         load_columns(k_pool, k_source, KEYS_FIRST, reach(0))
         load_columns(k_pool, k_source, reach(0), T)
         q_codes = held.tile([P, NQ], I32, name="q_codes", align_bytes=64)
+        nc.sync.dma_start(q_codes[:], q_words[0, 0].rearrange("p n t -> p (n t)").bitcast(I32))
         v_pool = held.tile([P, T], F32, name="v_pool", align_bytes=64)
 
-        ident = held.tile([P, P], F32, name="ident", align_bytes=64)
-        make_identity(nc, ident[:])
+        nc.gpsimd.affine_select(
+            out=ident[:],
+            in_=ident[:],
+            compare_op=ALU.not_equal,
+            fill=1.0,
+            base=0,
+            pattern=[[-1, P]],
+            channel_multiplier=1,
+        )
 
         ks_listed = held.tile([P, N], U8, name="ks_listed", align_bytes=64)
         nc.vector.tensor_copy(ks_listed[:], ks_pool[:, 0:T].indirect(offsets[:]))
-        for r in range(PACK):
+        for quadrant in range(PACK):
+            rows = ks_listed[KS_FIRST + PACK * quadrant : KS_FIRST + PACK * (quadrant + 1), :]
             nc.sync.dma_start(
-                planes[r:P:QUADRANT, 0:N].bitcast(I32), ks_listed[KS_FIRST + r : KS_END : PACK, :].bitcast(I32)
+                k_plane[QUADRANT * quadrant : QUADRANT * quadrant + PACK, 0:N].bitcast(I32), rows.bitcast(I32)
             )
-        nc.sync.dma_start(q_codes[:], q_words[0, 0].rearrange("p n t -> p (n t)").bitcast(I32))
         load_columns(v_pool, vT, 0, reach(0))
         load_columns(v_pool, vT, reach(0), T)
 
@@ -104,8 +116,8 @@ def tile_attend_qpk_cap_srt_kernel(tc, q_words, q_scales, k_words, k_scales, vT,
         nc.vector.tensor_copy(vs_listed[0][:], vs_pool[:, 0 : reach(0)].indirect(slots(0)))
         nc.scalar.activation(vs_listed[1][:], vs_pool[:].indirect(slots(1)), ACT.Copy)
         vs_row = held.tile([P, P, PASSES, PACK], F32, name="vs_row", tag="vs_row", align_bytes=64)
-        for g, place in enumerate((nc.vector.tensor_copy, nc.scalar.copy)):
-            place(
+        for g in range(PASSES):
+            nc.scalar.copy(
                 vs_row[LAST_QUADRANT:P, :, g, :].rearrange("r (b j) (u h) -> r b j u h", j=8, u=2),
                 vs_listed[g][LAST_QUADRANT:P, :].rearrange("r (b u j h) -> r b j u h", u=2, j=8, h=2),
             )
@@ -123,7 +135,7 @@ def tile_attend_qpk_cap_srt_kernel(tc, q_words, q_scales, k_words, k_scales, vT,
                 nc.tensor.matmul_mx(
                     out=score[:],
                     lhsT=q_codes[:].bitcast(FP8X4),
-                    lhsT_scale=q_plane,
+                    lhsT_scale=q_plane[:, 0:NQ],
                     rhs=k_listed[:, c - lo : c - lo + HALF].bitcast(FP8X4),
                     rhs_scale=k_plane[:, c : c + HALF],
                     start=True,
@@ -178,12 +190,10 @@ def tile_attend_qpk_cap_srt_kernel(tc, q_words, q_scales, k_words, k_scales, vT,
             v_turned.append(bank)
 
         weights = held.tile([P, N], BF16, name="weights", align_bytes=64)
-        inv_sum = held.tile([P, 1], F32, name="inv_sum", tag="vs_row", align_bytes=64)
-        nc.vector.reciprocal(inv_sum[:], row_sum[:])
         v_grouped = []
         pieces = (((0, DV),), ((0, DV // 2), (DV // 2, DV)))
         for g in range(PASSES):
-            grouped = held.tile([P, PASS], BF16, name="v_grouped%d" % g, align_bytes=64)
+            grouped = held.tile([P, PASS], BF16, name="v_grouped%d" % g, tag="v_grouped%d" % g, align_bytes=64)
             for lo, hi in pieces[g]:
                 nc.scalar.copy(
                     grouped[:].bitcast(F32).rearrange("s (e u) -> s e u", u=2)[:, lo:hi],
@@ -210,6 +220,9 @@ def tile_attend_qpk_cap_srt_kernel(tc, q_words, q_scales, k_words, k_scales, vT,
                     in_=v_grouped[g][:, PACK * lo : PACK * hi],
                 )
 
+        inv_sum = held.tile([P, 1], F32, name="inv_sum", tag="v_grouped1", align_bytes=64)
+        nc.vector.reciprocal(inv_sum[:], row_sum[:])
+
         acc = psum.tile([P, DV], F32, name="acc", tag="score0")
         for g in range(PASSES):
             nc.tensor.matmul_mx(
@@ -223,5 +236,5 @@ def tile_attend_qpk_cap_srt_kernel(tc, q_words, q_scales, k_words, k_scales, vT,
             )
 
         result = held.tile([P, DV], F32, name="result", align_bytes=64)
-        nc.scalar.activation(result[:], acc[:], ACT.Copy, scale=inv_sum[:])
+        nc.vector.tensor_scalar(result[:], acc[:], inv_sum[:], None, ALU.mult)
         nc.sync.dma_start(out[0], result[:])

from contextlib import ExitStack

import concourse.mybir as mybir

P = 128
T = 4096
N = 1024
D = 512
DV = 128
NQ = 128
CAP = 2.0
PACK = 4
PASS = P * PACK
PASSES = N // PASS
HALF = PASS // 2
LIST_COLS = PASS // 16
SCALE_ROWS = 16
QUADRANT = 32

KS_END = 64
KS_FIRST = KS_END - SCALE_ROWS
VS_ROW = P - 1
LAST_QUADRANT = P - QUADRANT
VS_FILL_VECTOR = 608
KEYS_FIRST = 1536
SPARE = 4

FLOPS = 2 * NQ * N * (D + DV)

F32 = mybir.dt.float32
BF16 = mybir.dt.bfloat16
I32 = mybir.dt.int32
U32 = mybir.dt.uint32
U16 = mybir.dt.uint16
U8 = mybir.dt.uint8
FP8X4 = mybir.dt.float8_e4m3fn_x4
ACT = mybir.ActivationFunctionType
ALU = mybir.AluOpType


def tile_attend_qpk_cap_srt_kernel(tc, q_words, q_scales, k_words, k_scales, vT, vs, offs, out):
    nc = tc.nc
    with ExitStack() as ctx:
        held = ctx.enter_context(tc.tile_pool(name="held", bufs=1))
        psum = ctx.enter_context(tc.psum_pool(name="psum", bufs=1))

        offsets = held.tile([P, N // 16], U16, name="offsets")

        def reach(g):
            return T - (N - (g + 1) * PASS)

        def slots(g):
            return offsets[:, g * LIST_COLS : (g + 1) * LIST_COLS]

        def pass_cols(g):
            return slice(g * PASS, (g + 1) * PASS)

        ident = held.tile([P, P], F32, name="ident", align_bytes=64)
        zero = held.tile([P, 1], F32, name="zero")
        nc.gpsimd.memset(zero[:], 0.0)
        nc.scalar.activation(ident[:], zero[:].to_broadcast([P, P]), ACT.Copy)

        ks_pool = held.tile([P, T + SPARE], U8, name="ks_pool", align_bytes=64)
        k_plane = held.tile([P, N + SPARE], U8, name="k_plane", align_bytes=64)
        q_plane = held.tile([P, NQ + SPARE], U8, name="q_plane", align_bytes=64)
        vs_pool = held.tile([P, T], F32, name="vs_pool", align_bytes=64)
        nc.vector.memset(q_plane[:].bitcast(I32), 0)
        nc.vector.memset(k_plane[:].bitcast(I32), 0)
        nc.vector.memset(ks_pool[0:KS_FIRST, :].bitcast(I32), 0)
        nc.gpsimd.memset(ks_pool[KS_END:P, 0:T].bitcast(I32), 0)
        nc.vector.memset(vs_pool[0:VS_ROW, 0:1], 0.0)
        nc.vector.memset(vs_pool[0:VS_ROW, 1:VS_FILL_VECTOR], 0.0)
        nc.gpsimd.memset(vs_pool[0:VS_ROW, VS_FILL_VECTOR : reach(0)], 0.0)
        nc.gpsimd.memset(vs_pool[0:VS_ROW, reach(0) : T], 0.0)

        def load_columns(pool_tile, source, lo, hi):
            nc.sync.dma_start(pool_tile[:, lo:hi], source[:, lo:hi])

        k_pool = held.tile([P, T], I32, name="k_pool", align_bytes=64)
        k_source = k_words[0].rearrange("p n t -> p (n t)").bitcast(I32)
        nc.sync.dma_start(ks_pool[KS_FIRST:KS_END, 0:T].bitcast(I32), k_scales[0].bitcast(I32))
        nc.sync.dma_start(offsets[:], offs)
        load_columns(k_pool, k_source, 0, KEYS_FIRST)
        nc.sync.dma_start(vs_pool[VS_ROW:P, :], vs[0:1, :])
        for r in range(PACK):
            nc.sync.dma_start(
                q_plane[r:P:QUADRANT, 0:NQ].bitcast(I32), q_scales[0, 0, r:SCALE_ROWS:PACK, :].bitcast(I32)
            )
        load_columns(k_pool, k_source, KEYS_FIRST, reach(0))
        load_columns(k_pool, k_source, reach(0), T)
        q_codes = held.tile([P, NQ], I32, name="q_codes", align_bytes=64)
        nc.sync.dma_start(q_codes[:], q_words[0, 0].rearrange("p n t -> p (n t)").bitcast(I32))
        v_pool = held.tile([P, T], F32, name="v_pool", align_bytes=64)

        nc.gpsimd.affine_select(
            out=ident[:],
            in_=ident[:],
            compare_op=ALU.not_equal,
            fill=1.0,
            base=0,
            pattern=[[-1, P]],
            channel_multiplier=1,
        )

        ks_listed = held.tile([P, N], U8, name="ks_listed", align_bytes=64)
        nc.vector.tensor_copy(ks_listed[:], ks_pool[:, 0:T].indirect(offsets[:]))
        for quadrant in range(PACK):
            rows = ks_listed[KS_FIRST + PACK * quadrant : KS_FIRST + PACK * (quadrant + 1), :]
            nc.sync.dma_start(
                k_plane[QUADRANT * quadrant : QUADRANT * quadrant + PACK, 0:N].bitcast(I32), rows.bitcast(I32)
            )
        load_columns(v_pool, vT, 0, reach(0))
        load_columns(v_pool, vT, reach(0), T)

        vs_listed = [held.tile([P, PASS], F32, name="vs_listed%d" % g, align_bytes=64) for g in range(PASSES)]
        nc.vector.tensor_copy(vs_listed[0][:], vs_pool[:, 0 : reach(0)].indirect(slots(0)))
        nc.scalar.activation(vs_listed[1][:], vs_pool[:].indirect(slots(1)), ACT.Copy)
        vs_row = held.tile([P, P, PASSES, PACK], F32, name="vs_row", tag="vs_row", align_bytes=64)
        for g in range(PASSES):
            nc.scalar.copy(
                vs_row[LAST_QUADRANT:P, :, g, :].rearrange("r (b j) (u h) -> r b j u h", j=8, u=2),
                vs_listed[g][LAST_QUADRANT:P, :].rearrange("r (b u j h) -> r b j u h", u=2, j=8, h=2),
            )
        vs_slot = held.tile([P, PASSES, PACK], F32, name="vs_slot", tag="vs_slot", align_bytes=64)
        nc.sync.dma_start(vs_slot[:].rearrange("s g t -> s (g t)"), vs_row[VS_ROW:P].rearrange("r s g t -> r (s g t)"))

        tanh_all = held.tile([P, N], F32, name="tanh_all", align_bytes=64)
        k_window = k_pool[:].bitcast(U32)
        for lo, hi, tokens in ((0, PASS, reach(0)), (PASS, PASS + HALF, T), (PASS + HALF, N, T)):
            k_listed = held.tile([P, hi - lo], I32, name="k_listed%d" % lo, align_bytes=64)
            listed = offsets[:, lo * LIST_COLS // PASS : hi * LIST_COLS // PASS]
            nc.vector.tensor_copy(k_listed[:].bitcast(U32), k_window[:, 0:tokens].indirect(listed))
            for c in range(lo, hi, HALF):
                score = psum.tile([P, HALF], F32, name="score%d" % c, tag="score%d" % c)
                nc.tensor.matmul_mx(
                    out=score[:],
                    lhsT=q_codes[:].bitcast(FP8X4),
                    lhsT_scale=q_plane[:, 0:NQ],
                    rhs=k_listed[:, c - lo : c - lo + HALF].bitcast(FP8X4),
                    rhs_scale=k_plane[:, c : c + HALF],
                    start=True,
                    stop=True,
                )
                nc.scalar.activation(tanh_all[:, c : c + HALF], score[:], ACT.Tanh, scale=1.0 / CAP)

        neg_c = held.tile([P, N], F32, name="neg_c", align_bytes=64)
        least = [held.tile([P, 1], F32, name="least%d" % g) for g in range(PASSES)]
        for g in range(PASSES):
            nc.vector.tensor_scalar(
                neg_c[:, pass_cols(g)],
                tanh_all[:, pass_cols(g)],
                -CAP,
                least[g - 1][:] if g else None,
                ALU.mult,
                ALU.min,
                accum_out=least[g][:],
            )
        neg_m = least[PASSES - 1][:]

        p_turned = []
        sums = held.tile([P, 2 * PASSES], F32, name="sums")
        for g in range(PASSES):
            bank = psum.tile([P, PACK, NQ], F32, name="p_turned%d" % g)
            by_place = neg_c[:, pass_cols(g)].rearrange("q (b u j h) -> q u h b j", u=2, j=8, h=2)
            for u in range(2):
                p = held.tile([P, HALF], F32, name="p%d%d" % (g, u), align_bytes=64)
                nc.scalar.activation(
                    p[:].rearrange("q (h b j) -> q h b j", h=2, j=8),
                    by_place[:, u],
                    ACT.Exp,
                    bias=neg_m,
                    scale=-1.0,
                    accum_out=sums[:, 2 * g + u : 2 * g + u + 1],
                )
                for h in range(2):
                    nc.tensor.transpose(bank[:, 2 * u + h, :], p[:, h * P : (h + 1) * P], ident[:])
            p_turned.append(bank)
        row_sum = held.tile([P, 1], F32, name="row_sum")
        nc.scalar.activation(sums[:], sums[:], ACT.Identity, accum_out=row_sum[:])

        v_turned = []
        for g in range(PASSES):
            v_pairs = held.tile([P, PASS], BF16, name="v_pairs%d" % g, align_bytes=64)[:]
            nc.vector.tensor_copy(
                v_pairs.rearrange("e (u b x) -> e b u x", u=2, x=16), v_pool[:, 0 : reach(g)].indirect(slots(g))
            )
            bank = psum.tile([P, 2, DV], F32, name="v_turned%d" % g)
            for u in range(2):
                nc.tensor.transpose(bank[:, u, :], v_pairs.bitcast(F32)[:, u * P : (u + 1) * P], ident[:])
            v_turned.append(bank)

        weights = held.tile([P, N], BF16, name="weights", align_bytes=64)
        v_grouped = []
        pieces = (((0, DV),), ((0, DV // 2), (DV // 2, DV)))
        for g in range(PASSES):
            grouped = held.tile([P, PASS], BF16, name="v_grouped%d" % g, tag="v_grouped%d" % g, align_bytes=64)
            for lo, hi in pieces[g]:
                nc.scalar.copy(
                    grouped[:].bitcast(F32).rearrange("s (e u) -> s e u", u=2)[:, lo:hi],
                    v_turned[g][:].rearrange("s u e -> s e u")[:, lo:hi],
                )
            v_grouped.append(grouped)
            nc.vector.tensor_tensor(
                weights[:, pass_cols(g)].rearrange("s (q t) -> s q t", t=PACK),
                p_turned[g][:].rearrange("s t q -> s q t"),
                vs_slot[:, g, :].unsqueeze(1).to_broadcast([P, NQ, PACK]),
                ALU.mult,
            )

        w_codes = held.tile([P, PASSES, NQ], U32, name="w_codes", align_bytes=64)
        v_codes = held.tile([P, PASSES, DV], U32, name="v_codes", align_bytes=64)
        w_plane = held.tile([P, PASSES, NQ], U8, name="w_plane", align_bytes=64)
        v_plane = held.tile([P, PASSES, DV], U8, name="v_plane", align_bytes=64)
        for g in range(PASSES):
            nc.vector.quantize_mx(out=w_codes[:, g, :].bitcast(FP8X4), scales=w_plane[:, g, :], in_=weights[:, pass_cols(g)])
            for lo, hi in pieces[g]:
                nc.vector.quantize_mx(
                    out=v_codes[:, g, lo:hi].bitcast(FP8X4),
                    scales=v_plane[:, g, lo:hi],
                    in_=v_grouped[g][:, PACK * lo : PACK * hi],
                )

        inv_sum = held.tile([P, 1], F32, name="inv_sum", tag="v_grouped1", align_bytes=64)
        nc.vector.reciprocal(inv_sum[:], row_sum[:])

        acc = psum.tile([P, DV], F32, name="acc", tag="score0")
        for g in range(PASSES):
            nc.tensor.matmul_mx(
                out=acc[:],
                lhsT=w_codes[:, g, :].bitcast(FP8X4),
                lhsT_scale=w_plane[:, g, :],
                rhs=v_codes[:, g, :].bitcast(FP8X4),
                rhs_scale=v_plane[:, g, :],
                start=(g == 0),
                stop=(g == PASSES - 1),
            )

        result = held.tile([P, DV], F32, name="result", align_bytes=64)
        nc.vector.tensor_scalar(result[:], acc[:], inv_sum[:], None, ALU.mult)
        nc.sync.dma_start(out[0], result[:])
